import numpy as np, ml_dtypes
CORES = [40,41,42,43,44,45,46,47]
N = 8
import mx_ref
BF = ml_dtypes.bfloat16
def pick(q, e):
    c = np.concatenate([q[0].reshape(128, -1, 4), np.zeros((128, 1, 4), np.uint8)], axis=1); s = np.concatenate([q[1], np.ones((16, 1), np.uint8)], axis=1)
    return (np.ascontiguousarray(c[:, e].reshape(128, -1)), np.ascontiguousarray(s[:, e]))
def join(*qs):
    return (np.concatenate([q[0] for q in qs], axis=1), np.concatenate([q[1] for q in qs], axis=1))
def put(q, e, v):
    c, s = q[0].reshape(128, -1, 4).copy(), q[1].copy(); c[:, e] = v[0].reshape(128, -1, 4); s[:, e] = v[1]
    return (c.reshape(128, -1), s)
def pk(c, s):
    return (np.ascontiguousarray(c), mx_ref.live(s))
def emit(q):
    return q[0], q[1]
def decode(q):
    o = []
    for b in range(4):
        e = np.zeros((128, 128, 4), np.float32); e[np.arange(128), np.arange(128), b] = 1
        o.append(mx_ref.matmul(mx_ref.quantize(e.reshape(128, 512).astype(BF)), q))
    return np.stack(o, axis=2).reshape(128, -1)
def cut(t, i, w=512):
    return t[:, w * i:w * i + w]
def f(rng, *shape):
    return mx_ref.flush((rng.standard_normal(shape, dtype=np.float32) * np.exp2(rng.integers(-2, 3, shape[:-1] + (1,)))).astype(BF))
def wide(rng, *shape, cols=0):
    v = rng.standard_normal(shape, dtype=np.float32) * np.exp2(rng.integers(-12, 13, shape)).astype(np.float32)
    if cols: v *= np.repeat(np.exp2(rng.integers(-cols, cols + 1, shape[:-2] + (1, shape[-1] // 4))) * (rng.random(shape[:-2] + (1, shape[-1] // 4)) > 0.0625), 4, axis=-1).astype(np.float32)
    return mx_ref.flush(v.astype(BF))
P, O = 256, 2
PART = [1, 4]
def keep(v):
    v = v.astype(np.float32)
    v[np.abs(v) < np.float32(2.0 ** -16)] = 0
    return v.astype(BF)
def astile(m):
    return np.ascontiguousarray(m.reshape(128, 4, -1).transpose(0, 2, 1)).reshape(128, -1)
def setup_inputs(rng):
    return {"x": keep(f(rng, N, 128, 4 * P)), "u": f(rng, N, 128, 512), "w": f(rng, N, 128, 512 * O)}
def setup_inputs_spread(rng):
    return {**setup_inputs(rng), "x": keep(wide(rng, N, 128, 4 * P, cols=6)), "u": wide(rng, N, 128, 512)}
def setup_inputs_ties(rng):
    d, xs, bare = setup_inputs(rng), [], int(rng.integers(0, N))
    for r in range(N):
        which = rng.permutation(np.concatenate([np.zeros(7 * P // 8, int), rng.integers(1, 6, P // 8)]))
        v = np.array(f(rng, 128, 24)).reshape(128, 6, 4)
        if r == bare: v[:, 0] = 0
        xs.append(keep(v[:, which].reshape(128, -1)))
    return {**d, "x": np.stack(xs)}
def setup_inputs_near(rng):
    d, xs, us = setup_inputs(rng), [], np.array(f(rng, N, 128, 512))
    H, K = P // 2, P // 4
    rows = np.setdiff1d(np.arange(480), [0, 4, 32])
    R = len(rows)
    for r in range(N):
        at = np.concatenate([[P - 1], rng.permutation(np.arange(1, P - 1)), [0]])
        pair, rest = np.sort(at[:H].reshape(K, 2), axis=1), at[H:]
        base = np.zeros((512, K))
        base[rows] = np.stack([rng.permutation(R) % 4 + 4 for j in range(K)], axis=1) * rng.choice([-1.0, 1.0], (R, K))
        base[[0, 4, 32]] = 4
        m = np.zeros((512, P))
        m[:, pair[:, 0]] = base
        m[:, pair[:, 1]] = base
        m[480, pair[:, 0]] = 2.0 ** -5
        m[480, pair[:, 1]] = 2.0 ** -4
        m[484, pair[:, 0]] = 2.0 ** -5
        v = base[:, rng.permutation(np.repeat(np.arange(K), 2))]
        v[rows] *= np.stack([np.where(rng.permutation(R) < R // 4, -1.0, 1.0) for j in range(H)], axis=1)
        v[0, :K] = -4
        v[480] = 2.0 ** -5
        m[:, rest] = v
        xs.append(astile(m).astype(np.float32).astype(BF))
        us[r, :, :4] = 0
        us[r, 8, 0] = 2.0 ** 10
        us[r, 1, 0] = 2.0 ** -11
        us[r, 0, 0] = -2.0 ** -13
    return {**d, "x": np.stack(xs), "u": us}
def setup_inputs_far(rng):
    d, xs, us = setup_inputs(rng), [], []
    H, s = P // 2, rng.choice([-1.0, 1.0], (512, 1))
    for r in range(N):
        at, m = rng.permutation(P), np.zeros((512, P))
        m[:, at[:H]] = np.where(rng.random((512, H)) < 0.8, 1.0, 0.875)
        m[:, at[0]] = np.where(rng.random(512) < 0.9, 0.875, 0.75)
        m[:, at[H:]] = -np.where(rng.random((512, H)) < 0.5, 0.625, 0.75)
        xs.append(astile(m * s * 2.0 ** 28).astype(np.float32).astype(BF))
        us.append(astile(np.where(rng.random((512, 128)) < 0.5, 1.5, 1.75) * s * 2.0 ** 29).astype(np.float32).astype(BF))
    return {**d, "x": np.stack(xs), "u": np.stack(us)}
def setup_inputs_later(rng):
    d, xs = setup_inputs(rng), []
    H, K = P // 2, P // 4
    low = [r for r in range(N) if r < r ^ PART[0]]
    size = np.ones(N)
    for r in rng.permutation(low)[:len(low) // 2]: size[r ^ PART[0]] = 64
    for r in range(N):
        at, m = rng.permutation(P), np.zeros((512, P))
        z = rng.standard_normal((512, H))
        m[:, at[:H]] = z
        m[:, at[H:H + K]] = 0.6 * z[:, rng.integers(0, H, K)] + 0.05 * rng.standard_normal((512, K))
        m[:, at[H + K:]] = 0.45 * rng.standard_normal((512, P - H - K))
        xs.append(keep(astile(m * size[r])))
    return {**d, "x": np.stack(xs)}
def check_inputs(d):
    b = []
    for k, lo, hi in (("x", -20, 28), ("u", -30, 30), ("w", -30, 30)):
        v = np.abs(d[k].astype(np.float32))
        if not (np.isfinite(v).all() and ((v == 0) | (v >= 2.0 ** lo) & (v <= 2.0 ** hi)).all()): b.append("a value of " + k)
    return b
def gram(q):
    n = q[1].shape[1]
    g = np.zeros((n, n), np.float32)
    for i in range(0, n, 128):
        e = np.arange(i, i + 128)
        e[e >= n] = -1
        z = mx_ref.matmul(pick(q, e), pick(q, np.arange(i, n)))[:n - i]
        g[i:i + 128, i:] = z
        g[i:, i:i + 128] = z.T
    return g + np.float32(0)
def score(q, k):
    n = q[1].shape[1]
    e = np.arange(n + -n % 128)
    e[n:] = -1
    return np.concatenate([mx_ref.matmul(pick(q, e[i:i + 128]), pick(k, np.arange(4))) for i in range(0, len(e), 128)])[:n] + np.float32(0)
def high(s, k):
    return np.sort(np.argsort(-s, kind="stable")[:k])
def opened(qs):
    q, out, i = join(*qs), [], 0
    n = q[1].shape[1]
    e = np.arange(n + -n % 4)
    e[n:] = -1
    v = decode(pick(q, e)).reshape(128, -1, 4)
    for p in qs:
        k = p[1].shape[1]
        out.append(v[:, i:i + k])
        i += k
    return out
def anew(v):
    n = v.shape[1]
    v = np.concatenate([v, np.zeros((128, -n % 4, 4), np.float32)], axis=1)
    return pick(mx_ref.quantize(np.ascontiguousarray(v.reshape(128, -1).astype(BF))), np.arange(n))
def reference(x, u, w):
    y, pa = np.zeros((N, 128, O * P), np.float32), np.zeros((N, 1, P + P // 2 + P // 4), np.float32)
    oc, osc = np.zeros((N, 128, 4 * P), np.uint8), np.zeros((N, 16, P), np.uint8)
    uq = [mx_ref.quantize(np.ascontiguousarray(u[r])) for r in range(N)]
    front = [mx_ref.quantize(np.ascontiguousarray(x[r])) for r in range(N)]
    fronts, kin, ways, at = [], [], [], 0
    for l in range(3):
        n = P >> l
        who, done, kept, way = [], [], [], []
        for r in range(N):
            g = gram(front[r])
            piv = high(np.diagonal(g), n // 2)
            non = np.setdiff1d(np.arange(n), piv)
            par = piv[np.argmax(g[piv][:, non], axis=0)]
            pa[r, 0, at + piv] = piv
            pa[r, 0, at + non] = par
            have, first = np.unique(par, return_index=True)
            who.append((non, par, have, non[first]))
        v = opened([pick(front[r], np.concatenate([who[r][0], who[r][2]])) for r in range(N)])
        for r in range(N):
            non, par, have, kid = who[r]
            dn, dp = v[r][:, :n // 2], v[r][:, n // 2:]
            new = anew(dn - np.float32(0.5) * dp[:, np.searchsorted(have, par)])
            done.append(put(front[r], non, new))
            kept.append((have, kid, dp))
            if l < 2:
                go = non[high(score(new, uq[r])[:, l], n // 4)]
                way.append((np.setdiff1d(non, go), go))
        at += n
        fronts.append(done)
        kin.append(kept)
        ways.append(way)
        if l < 2: front = [join(pick(done[r], way[r][0]), pick(done[r ^ PART[l]], way[r ^ PART[l]][1])) for r in range(N)]
    below = None
    for l in (2, 1, 0):
        n = P >> l
        now = fronts[l]
        if l < 2:
            k = n // 4
            for r in range(N):
                stay, go = ways[l][r]
                now[r] = put(now[r], stay, pick(below[r], np.arange(k)))
                now[r] = put(now[r], go, pick(below[r ^ PART[l]], np.arange(k, 2 * k)))
        v = opened([pick(now[r], kin[l][r][1]) for r in range(N)])
        for r in range(N):
            have, kid, dp = kin[l][r]
            now[r] = put(now[r], have, anew((dp + v[r]) * np.float32(0.5)))
        below = now
    for r in range(N):
        for o in range(O):
            y[r, :, o * P:o * P + P] = mx_ref.matmul(mx_ref.quantize(np.ascontiguousarray(cut(w[r], o))), below[r])
        oc[r], osc[r] = emit(below[r])
    return {"y": y, "oc": oc, "osc": osc, "pa": pa}

@@ -1,0 +1,603 @@
+from concourse.mybir import dt, AluOpType, ActivationFunctionType
+
+OP = AluOpType
+FN = ActivationFunctionType
+PART = [1, 4]
+TW = 136
+BIG = 2.0 ** 90
+TINY = 2.0 ** -100
+LOW = -1.0e29
+
+PAIRS = {"W0": 512, "W1": 320, "W2": 384, "V0": 128, "PAR0": 128, "PR0": 128, "PAR1": 128, "PR1": 128, "PAR2": 128,
+         "E0": 128, "E1": 128, "L0": 128, "SN1": 64, "SND": 64, "FIN": 256, "UQ": 256, "WQ": 256, "KQ": 1920,
+         "CQ": 256, "TQ": 1440}
+SCRATCH = {}
+for _n, _w in PAIRS.items():
+    SCRATCH["q" + _n] = ("sbuf", [128, _w], "float8_e4m3fn_x4")
+    SCRATCH["s" + _n] = ("sbuf", [128, _w], "uint8")
+for _n, _w in {"xt": 1024, "wt": 1024, "ut": 16, "ub": 1024, "zb": 520, "eb": 2080, "kt": 3584, "ct": 1024, "tx": 4 * TW,
+               "ty": 4 * TW, "ts": 512, "ht": 512, "tn": 128, "tp": 128, "tc": 128, "df": 256, "junk": 4096}.items():
+    SCRATCH[_n] = ("sbuf", [128, _w], "bfloat16")
+for _n, _w in {"zf": 256, "idn": 128, "ki": TW, "k2": 8, "ka": 8, "tmp": 320, "xs": 320, "rr": 256, "zs": 256, "gs": 128, "gd": 128,
+               "gm": 256, "sc": 256, "fl": 256, "eqi": 256, "ea": 128, "ebq": 128, "col": 48, "cst": 8, "par": 256,
+               "prow": 128, "ysb": 512, "m16": 128}.items():
+    SCRATCH[_n] = ("sbuf", [128, _w], "float32")
+SCRATCH["mi"] = ("sbuf", [128, 128], "int32")
+SCRATCH["mj"] = ("sbuf", [128, 128], "int32")
+SCRATCH["off"] = ("sbuf", [128, 96], "uint16")
+SCRATCH["ofr"] = ("sbuf", [128, 8], "uint16")
+SCRATCH["ps"] = ("psum", [128, 4096], "float32")
+DMAS = ["dx0", "dx1", "du", "dw", "dp0", "dp1", "dp2", "doc", "ds0", "ds1", "ds2", "ds3", "dy0", "dy1"]
+SEMAPHORES = ["cv", "ca", "cp", "cg", "arr0", "arr1", "arr2", "arr3", "snt"] + DMAS
+
+K_A, K_16, K_SA, K_R, K_B, K_SB, K_C, K_E1, K_EH = 0, 1, 2, 3, 4, 5, 6, 7, 11
+BA, BB, BC, BD = 4, 5, 6, 7
+
+
+def V(name, c0, c1, step=1, p0=0, p1=128):
+    return (name, p0, p1, c0, c1, step)
+
+
+def PS(bank, c0, c1, step=1):
+    return V("ps", 512 * bank + c0, 512 * bank + c1, step)
+
+
+def clash(a, b):
+    if a[0] != b[0]:
+        return False
+    if a[0] == "ps":
+        return a[3] // 512 == b[3] // 512
+    if a[2] <= b[1] or b[2] <= a[1] or a[4] <= b[3] or b[4] <= a[3]:
+        return False
+    if a[5] == b[5] and a[5] > 1:
+        return (a[3] - b[3]) % a[5] == 0
+    return True
+
+
+def rank_program(g, core, T, topo):
+    rank = T.rank_of(core)
+    if rank is None:
+        return
+    ops = []
+    spare = [0]
+    queue = {"v": g.vector, "a": g.scalar, "p": g.tensor, "g": g, "s": g.sync}
+
+    def ap(v):
+        if not isinstance(v, tuple):
+            return v
+        if v[5] == 1:
+            return T[v[0]][v[1]:v[2], v[3]:v[4]]
+        return T[v[0]][v[1]:v[2], v[3]:v[4]:v[5]]
+
+    def views(*xs):
+        return [x for x in xs if isinstance(x, tuple)]
+
+    def add(q, reads, writes, fn, sem=None, kind="c"):
+        ops.append({"q": q, "r": reads, "w": writes, "fn": fn, "sem": sem, "kind": kind})
+
+    def memset(o, c):
+        add("v", [], [o], lambda: g.vector.memset(ap(o), c))
+
+    def copy(o, i):
+        add("v", [i], [o], lambda: g.vector.tensor_copy(ap(o), ap(i)))
+
+    def tt(o, a, b, op):
+        add("v", [a, b], [o], lambda: g.vector.tensor_tensor(ap(o), ap(a), ap(b), op))
+
+    def ts(o, a, s1, op0, s2=None, op1=None):
+        if op1 is None:
+            add("v", views(a, s1), [o], lambda: g.vector.tensor_scalar(ap(o), ap(a), ap(s1), None, op0))
+        else:
+            add("v", views(a, s1, s2), [o], lambda: g.vector.tensor_scalar(ap(o), ap(a), ap(s1), ap(s2), op0, op1))
+
+    def scan(o, a, b, init, op0, op1):
+        add("v", views(a, b, init), [o], lambda: g.vector.tensor_tensor_scan(ap(o), ap(a), ap(b), ap(init), op0, op1))
+
+    def turn(o, i):
+        add("v", [i], [o], lambda: g.vector.transpose(ap(o), ap(i)))
+
+    def act(o, i, fn, bias=None, scale=None, acc=None):
+        kw = {}
+        if bias is not None:
+            kw["bias"] = bias
+        if scale is not None:
+            kw["scale"] = scale
+        if acc is not None:
+            kw["accum_out"] = acc
+        if o[0] == "junk":
+            o = V("junk", spare[0], spare[0] + o[4])
+            spare[0] = o[4]
+        add("a", views(i, bias, scale), views(o, acc),
+            lambda: g.scalar.activation(ap(o), ap(i), fn, **{k: ap(x) for k, x in kw.items()}))
+
+    def pool(reads, o, fn):
+        turn_ = V("pool", 0, 1)
+        if o[2] - o[1] < 128:
+            add("g", reads, [o, turn_], fn)
+        else:
+            add("g", reads + [turn_], [o], fn)
+
+    def iota(o, pat, base, cm):
+        if o[0] == "mi":
+            pool([], o, lambda: g.iota(ap(o), pat, base, cm))
+        else:
+            pool([], o, lambda: g.iota(ap(o), pat, base, cm, allow_small_or_imprecise_dtypes=True))
+
+    def sel(o, i, pat, op, fill, base, cm):
+        pool([i], o, lambda: g.affine_select(ap(o), ap(i), pat, op, fill, base, cm))
+
+    def pq(n, a, b):
+        return V("q" + n, a, b), V("s" + n, a, b)
+
+    def quant(n, a, b, tile):
+        q, s = pq(n, a, b)
+        add("v", [tile], [q, s], lambda: g.vector.quantize_mx(ap(q), ap(s), ap(tile)))
+
+    def mm(bank, w, x, start=True, stop=True):
+        qw, sw = pq(*w)
+        qx, sx = pq(*x)
+        o = PS(bank, 0, x[2] - x[1])
+        add("p", [qw, sw, qx, sx], [o],
+            lambda: g.tensor.matmul_mx(ap(o), ap(qw), ap(sw), ap(qx), ap(sx), start, stop))
+
+    def kq(slot):
+        return ("KQ", 128 * slot, 128 * slot + 128)
+
+    def pick(dst, win, o0, o1, lists="off"):
+        qd, sd = pq(*dst)
+        qw, sw = pq(*win)
+        of = V(lists, o0, o1)
+        add("v", [qw, of], [qd], lambda: g.vector.tensor_copy(
+            ap(qd).bitcast(dt.uint32), ap(qw).bitcast(dt.uint32).indirect(ap(of))))
+        add("a", [sw, of], [sd], lambda: g.scalar.activation(ap(sd), ap(sw).indirect(ap(of)), FN.Copy))
+
+    def dma(q, sem, reads, writes, out, in_):
+        add(q, reads, writes, lambda: queue[q].dma_start(out(), in_()), sem, "d")
+
+    def send(k, src, dst, peer_rank):
+        peer = T.cores[peer_rank]
+        rid, pid, _ = topo.addr(peer)
+        mask = topo.mask(core, peer)
+        qs, ss = pq(*src)
+        qd, sd = pq(*dst)
+        sem = T.sem["arr%d" % k]
+        add("g", [qs], [], lambda: g.remote_dma(ap(qd).bitcast(dt.uint8), ap(qs).bitcast(dt.uint8), sem, T.sem.snt,
+                                                pid, rid, mask), None, "r")
+        add("g", [ss], [], lambda: g.remote_dma(ap(sd), ap(ss), sem, T.sem.snt, pid, rid, mask), None, "r")
+        n = 2 * len(topo.engines(peer, core))
+        add(None, [], [qd, sd], None, ("arr%d" % k, n), "x")
+        return 2 * len(topo.engines(core, peer))
+
+    def send_list(k, src, dst, peer_rank):
+        peer = T.cores[peer_rank]
+        rid, pid, _ = topo.addr(peer)
+        add("g", [src], [], lambda: g.remote_dma(ap(dst), ap(src), T.sem["arr%d" % k], T.sem.snt, pid, rid,
+                                                 topo.mask(core, peer)), None, "r")
+        add(None, [], [dst], None, ("arr%d" % k, len(topo.engines(peer, core))), "x")
+        return len(topo.engines(core, peer))
+
+    def C(k):
+        return V("col", k, k + 1)
+
+    def K(k, p0=0, p1=128):
+        return V("cst", k, k + 1, 1, p0, p1)
+
+    def sub(tile, t, c0, c1, p0=0, p1=128):
+        return V(tile, 4 * c0 + t, 4 * c1, 4, p0, p1)
+
+    def whole(tile, c0, c1):
+        return V(tile, 4 * c0, 4 * c1)
+
+    def kfill(slot, t, c, c0=0, c1=128, p0=0, p1=128):
+        memset(sub("kt", t, 128 * slot + c0, 128 * slot + c1, p0, p1), c)
+
+    def afill(slot, t, c):
+        act(sub("kt", t, 128 * slot, 128 * slot + 128), V("zf", 0, 128), FN.Identity, c)
+
+    def kquant(slot):
+        if slot < K_E1:
+            quant("KQ", 128 * slot, 128 * slot + 128, whole("kt", 128 * slot, 128 * slot + 128))
+        else:
+            h, b = divmod(slot - K_E1, 4)
+            at = 520 * (2 * h + b % 2) + (2 - b // 2 * 2)
+            quant("KQ", 128 * slot, 128 * slot + 128, V("eb", at, at + 512))
+
+    def count(r, n, bias, hi, tot):
+        if hi is not None:
+            act(V("junk", 0, n // 16), V(r, 15, n, 16), FN.Sign, bias, -1.0, hi)
+        act(V("junk", 0, n), V(r, 0, n), FN.Sign, bias, -1.0, tot)
+
+    def digits(tile, c0, c1, kc, hi, tot):
+        ts(sub(tile, 1, c0, c1), kc, tot, OP.mult, hi, OP.subtract)
+        act(sub(tile, 0, c0, c1), V("zf", 0, c1 - c0), FN.Identity, hi)
+
+    def carry(tile, slot, n, bank, o0, k):
+        quant("TQ", 160 * slot, 160 * slot + n, whole(tile, 0, n))
+        mm(bank, kq(K_16), ("TQ", 160 * slot, 160 * slot + 128))
+
+        def fin():
+            copy(V("off", o0, o0 + k), PS(bank, 0, k))
+        return fin
+
+    def row(slot, bank):
+        mm(bank, kq(K_R), ("TQ", 160 * slot + 8, 160 * slot + TW))
+
+    def opend(src, slot0, start):
+        for b in range(4):
+            mm(b, kq(slot0 + b), src, start, not start)
+
+    def anew(dst, half):
+        for b in range(4):
+            o, i = sub("ht", b, 0, 128), PS(b, 0, 128)
+            if b % 2 == 0:
+                act(o, i, FN.Copy, None, 0.5 if half else None)
+            elif half:
+                ts(o, i, 0.5, OP.mult)
+            else:
+                copy(o, i)
+        quant(*dst, whole("ht", 0, 128))
+
+    def diag(bank, at):
+        tt(V("tmp", at, at + 128), PS(bank, 0, 128), V("idn", 0, 128), OP.mult)
+        scan(V("xs", at, at + 160), V("tmp", at, at + 160), V("tmp", at, at + 160), 0.0, OP.max, OP.max)
+
+    def turns(at, to):
+        for a in range(4):
+            turn(V("rr", to + 32 * a, to + 32 * a + 32, 1, 0, 32), V("xs", at + 128, at + 160, 1, 32 * a, 32 * a + 32))
+
+    def ubuild(l):
+        for t in range(4):
+            act(sub("ub", t, 128 * l, 128 * l + 128), V("zf", 0, 128), FN.Identity, V("ut", 4 * l + t, 4 * l + t + 1))
+
+    KI = V("ki", 0, TW)
+    K8 = V("ki", 0, 8)
+    IDN = V("idn", 0, 128)
+    O_V, O_P0, O_L0, O_P1, O_L1, O_P2, O_S2, O_S1, O_S0 = 0, 8, 16, 24, 32, 40, 48, 56, 64
+    for h in range(2):
+        dma("s", "dx%d" % h, [], [V("xt", 512 * h, 512 * h + 512)],
+            lambda h=h: T.xt[:, 512 * h:512 * h + 512], lambda h=h: T.x[:, 512 * h:512 * h + 512])
+    dma("a", "du", [], [V("ut", 0, 8)], lambda: T.ut[:, 0:8], lambda: T.u[:, 0:8])
+    dma("s", "dw", [V("xt", 512, 1024)], [V("wt", 0, 1024)], lambda: T.wt[:, :], lambda: T.w[:, :])
+
+    memset(V("zf", 0, 256), 0.0)
+    memset(V("zb", 0, 520), 0.0)
+    sel(IDN, V("zf", 0, 128), [[-1, 128]], OP.not_equal, 1.0, 0, 1)
+    iota(V("mi", 0, 128), [[-1, 128]], 128, 1)
+    sel(V("tn", 0, 128), V("zb", 0, 128), [[-1, 128]], OP.is_ge, -TINY, 0, 1)
+    sel(V("ki", 8, TW), V("zf", 0, 128), [[-1, 128]], OP.not_equal, 0.0625, 0, 1)
+    sel(V("ka", 0, 8), V("zf", 0, 8), [[16, 8]], OP.is_gt, 0.0625, 0, -1)
+    iota(K(0), [[0, 1]], 0, 1)
+    iota(K(1), [[0, 1]], 128, 1)
+    sel(K8, V("ka", 0, 8), [[16, 8]], OP.is_ge, 0.0, 15, -1)
+    for j, (at, c) in enumerate(((2, 1.0), (3, 1.0), (2, -0.5), (3, -0.5))):
+        sel(V("eb", 520 * j, 520 * j + 520), V("zb", 0, 520), [[-1, 520]], OP.not_equal, c, at, 4)
+    sel(V("tp", 0, 128), V("zb", 0, 128), [[-1, 128]], OP.is_ge, TINY, 0, 1)
+    for h in range(2):
+        iota(K(4, 64 * h, 64 * h + 64), [[0, 1]], -1, -1)
+    for h in range(4):
+        iota(K(5, 32 * h, 32 * h + 32), [[0, 1]], -1, -1)
+    iota(V("par", 0, 256), [[1, 256]], 0, 0)
+    sel(V("tc", 0, 128, 1, 0, 64), V("tn", 0, 128, 1, 0, 64), [[-1, 128]], OP.is_gt, -BIG, 64, 0)
+    sel(V("tc", 0, 128, 1, 64, 128), V("tn", 0, 128, 1, 64, 128), [[1, 128]], OP.is_gt, -BIG, -63, 0)
+
+    memset(V("tmp", 128, 160), 0.0)
+    memset(V("tmp", 288, 320), 0.0)
+    memset(sub("ct", 2, 0, 256), 1.0)
+    memset(sub("ct", 3, 0, 256), 1.0)
+    for t, c in enumerate((-2.0 ** 30, -2.0 ** 30, 2.0 ** 30, -2.0 ** 22)):
+        kfill(K_A, t, c)
+    memset(whole("tx", 0, TW), 0.0)
+    ts(V("mj", 0, 128), V("mi", 0, 128), 15, OP.bitwise_and)
+    kquant(K_A)
+    ts(V("m16", 0, 128), V("mj", 0, 128), 0.0, OP.is_equal, 16.0, OP.mult)
+    kfill(K_SA, 0, -1.0, 0, 64)
+    kfill(K_SA, 0, 1.0, 64, 128)
+    memset(K(2, 0, 64), -63.0)
+    memset(K(2, 64, 128), 64.0)
+    for t in (1, 2, 3):
+        act(sub("kt", t, 128 * K_SA, 128 * K_SA + 128), V("zf", 0, 128), FN.Copy)
+    act(sub("kt", 3, 128 * K_R, 128 * K_R + 128), V("zf", 0, 128), FN.Copy)
+    act(sub("kt", 2, 128 * K_R, 128 * K_R + 128), IDN, FN.Copy, None, 16.0)
+    act(V("eqi", 128, 256), IDN, FN.Copy)
+    for t, c in enumerate((-2.0 ** 30, 0.0, 2.0 ** 29, -2.0 ** 22)):
+        afill(K_B, t, c)
+    for t, c in ((1, -256.0), (2, 0.0), (3, 0.0)):
+        afill(K_SB, t, c)
+    for h in range(4):
+        kfill(K_SB, 0, -1.0 if h % 2 == 0 else 1.0, 32 * h, 32 * h + 32)
+        memset(K(3, 32 * h, 32 * h + 32), -31.0 if h % 2 == 0 else 32.0)
+    kfill(K_R, 0, 16.0)
+    kfill(K_R, 1, 16.0)
+    for t in range(4):
+        act(sub("kt", t, 128 * K_16, 128 * K_16 + 128), V("m16", 0, 128), FN.Copy)
+    ubuild(0)
+
+    def gram0(h):
+        quant("W0", 128 + 128 * h, 256 + 128 * h, whole("xt", 128 * h, 128 * h + 128))
+        mm(BA + h, ("W0", 128 + 128 * h, 256 + 128 * h), ("W0", 128 + 128 * h, 256 + 128 * h))
+    d0, d1 = V("xs", 128, 129), V("xs", 288, 289)
+    gram0(0)
+    diag(BA, 0)
+    gram0(1)
+    turns(0, 0)
+    for b in (1, 2, 3):
+        act(V("rr", 0, 128, 1, 32 * b, 32 * b + 32), V("rr", 0, 128, 1, 0, 32), FN.Copy)
+    act(V("df", 0, 128), V("rr", 0, 128), FN.Identity, d0, -1.0)
+    diag(BB, 160)
+    turns(160, 128)
+    for b in (1, 2, 3):
+        act(V("rr", 128, 256, 1, 32 * b, 32 * b + 32), V("rr", 128, 256, 1, 0, 32), FN.Copy)
+    act(V("df", 128, 256), V("rr", 128, 256), FN.Identity, d1, -1.0)
+    ts(sub("ct", 1, 0, 128), V("rr", 0, 128), d1, OP.is_lt)
+    tt(sub("ct", 0, 0, 128), V("df", 0, 128), V("tn", 0, 128), OP.is_gt)
+    ts(sub("ct", 0, 128, 256), V("rr", 128, 256), d0, OP.is_le)
+    tt(sub("ct", 1, 128, 256), V("df", 128, 256), V("tn", 0, 128), OP.is_gt)
+    quant("CQ", 0, 256, whole("ct", 0, 256))
+    mm(BA, kq(K_A), ("CQ", 0, 256))
+    kquant(K_16)
+    ts(C(0), K(0), -1.0, OP.mult, -1.0, OP.add)
+    ts(V("fl", 0, 256), PS(BA, 0, 256), 0.0, OP.is_lt)
+    scan(V("sc", 0, 256), V("fl", 0, 256), V("zf", 0, 256), C(0), OP.add, OP.min)
+    act(V("zs", 0, 256), PS(BA, 0, 256), FN.Copy, None, 2.0 ** 40)
+    count("sc", 256, None, C(1), C(2))
+    for s in range(K_E1, K_E1 + 2):
+        kquant(s)
+    digits("tx", 0, TW, KI, C(1), C(2))
+    fin = carry("tx", 0, TW, BB, O_V, 8)
+    kquant(K_E1 + 2)
+    fin()
+    Q0 = ("W0", 128, 384)
+    pick(("V0", 0, 128), Q0, O_V, O_V + 8)
+    mm(BA, ("V0", 0, 128), Q0)
+    ubuild(1)
+    kquant(K_E1 + 3)
+    opend(("V0", 0, 128), K_E1, True)
+    tt(V("gm", 0, 256), PS(BA, 0, 256), V("zs", 0, 256), OP.min)
+    scan(V("sc", 0, 256), V("gm", 0, 256), V("gm", 0, 256), LOW, OP.max, OP.max)
+    count("sc", 256, V("sc", 255, 256), C(3), C(4))
+    for s in range(K_EH, K_EH + 3):
+        kquant(s)
+    digits("tx", 0, TW, KI, C(3), C(4))
+    fin = carry("tx", 1, TW, BB, O_P0, 8)
+    kquant(K_EH + 3)
+    fin()
+    pick(("PAR0", 0, 128), Q0, O_P0, O_P0 + 8)
+    opend(("PAR0", 0, 128), K_EH, False)
+    quant("UQ", 0, 128, whole("ub", 0, 128))
+    kquant(K_SA)
+    anew(("E0", 0, 128), False)
+    sent = send(0, ("E0", 0, 128), ("L0", 0, 128), rank ^ PART[0])
+
+    def choose(l, E, kw, thr, start, mask, hi, tot, slot, o0, gap):
+        u = ("UQ", 128 * l, 128 * l + 128)
+        mm(BC, u, E)
+        mm(BD, E, u)
+        gap(0)
+        if mask is None:
+            ts(V("df", 0, 128), PS(BC, 0, 128), PS(BD, 0, 1), OP.subtract)
+        else:
+            ts(V("df", 0, 128), PS(BC, 0, 128), PS(BD, 0, 1), OP.subtract, mask, OP.add)
+        tt(sub("ct", 0, 128, 256), V("df", 0, 128), V("tp", 0, 128), OP.is_lt)
+        quant("CQ", 128, 256, whole("ct", 128, 256))
+        mm(BA, kq(kw), ("CQ", 128, 256))
+        gap(1)
+        ts(V("fl", 0, 128), PS(BA, 0, 128), thr, OP.is_ge)
+        scan(V("sc", 0, 128), V("fl", 0, 128), V("zf", 0, 128), start, OP.add, OP.min)
+        count("sc", 128, None, hi, tot)
+        gap(2)
+        digits("tx", 0, TW, KI, hi, tot)
+        carry("tx", slot, TW, BB, o0, 8)()
+
+    def gap0(k):
+        if k == 0:
+            kquant(K_R)
+        if k == 1:
+            memset(whole("kt", 128 * K_C, 128 * K_C + 128), 0.0)
+        if k == 2:
+            memset(whole("ty", 0, TW), 0.0)
+    choose(0, ("E0", 0, 128), K_SA, K(2), K(4), None, C(5), C(6), 2, O_L0, gap0)
+    sent += send_list(3, V("off", O_L0, O_L0 + 4), V("ofr", 0, 4), rank ^ PART[0])
+    pick(("W1", 128, 192), ("E0", 0, 128), O_L0 + 4, O_L0 + 8)
+
+    def later(b):
+        ts(V("eqi", 0, 128), PS(BD, 0, 128), C(10 + b), OP.is_equal)
+        scan(V("sc", 0, 256), V("eqi", 0, 256), V("eqi", 0, 256), 0.0, OP.max, OP.max)
+        count("sc", 256, 1.0, C(26 + 2 * b), C(27 + 2 * b))
+
+    row(1, BC)
+    row(0, BD)
+    act(sub("ty", 2, 8, TW), IDN, FN.Copy, None, 16.0)
+    for b in range(2):
+        ts(V("ea", 0, 128), PS(BC, 0, 128), K(b), OP.is_equal)
+        ts(V("ebq", 0, 128), PS(BD, 0, 128), K(b), OP.is_equal)
+        if b == 0:
+            kquant(K_B)
+        else:
+            kquant(K_SB)
+        scan(V("sc", 0, 128), V("ea", 0, 128), V("ebq", 0, 128), 0.0, OP.max, OP.max)
+        act(V("junk", 0, 128), V("ebq", 0, 128), FN.Copy, None, None, C(8 + b))
+        count("sc", 128, 1.0, None, C(10 + b))
+    act(V("prow", 0, 128), PS(BC, 0, 128), FN.Copy)
+    row(2, BD)
+    later(0)
+
+    def front(F, tri, kw, hi, tot, slot, o0, PAR, E, after):
+        mm(BA, F, F)
+        opend(F, K_E1, True)
+        diag(BA, 0)
+        act(V("gs", 0, 128), PS(BA, 0, 128), FN.Copy, None, 2.0 ** -40)
+        sel(V("gd", 0, 128), V("gs", 0, 128), [[-1, 128]], OP.not_equal, 3.0 * 2.0 ** 27, 0, 1)
+        turns(0, 0)
+        for b in (2, 0, 3, 1):
+            o, i, d = V("df", 0, 128, 1, 32 * b, 32 * b + 32), V("rr", 0, 128, 1, 0, 32), V("xs", 128, 129, 1, 32 * b, 32 * b + 32)
+            if b >= 2:
+                act(o, i, FN.Identity, d, -1.0)
+            else:
+                ts(o, i, d, OP.subtract, -1.0, OP.mult)
+        tt(sub("ct", 0, 0, 128), V("df", 0, 128), V(tri, 0, 128), OP.is_gt)
+        quant("CQ", 0, 128, whole("ct", 0, 128))
+        mm(BB, kq(kw), ("CQ", 0, 128))
+        after(2)
+        tt(V("gm", 0, 128), PS(BB, 0, 128), V("gd", 0, 128), OP.min)
+        scan(V("sc", 0, 128), V("gm", 0, 128), V("gm", 0, 128), LOW, OP.max, OP.max)
+        count("sc", 128, V("sc", 127, 128), hi, tot)
+        after(3)
+        digits("ty", 0, TW, KI, hi, tot)
+        fin = carry("ty", slot, TW, BA, o0, 8)
+        after(0)
+        fin()
+        pick(PAR, F, o0, o0 + 8)
+        opend(PAR, K_EH, False)
+        after(1)
+        anew(E, False)
+
+    def after1(k):
+        if k == 2:
+            quant("UQ", 128, 256, whole("ub", 128, 256))
+        if k == 3:
+            memset(whole("ts", 0, 128), 0.0)
+        if k == 0:
+            ts(C(14), C(13), K(0), OP.is_equal, BIG, OP.mult)
+        if k == 1:
+            ts(sub("ct", 1, 128, 256), IDN, C(14), OP.mult, 1.0 / BIG, OP.mult)
+            ts(C(15), C(13), K(0), OP.not_equal)
+    F1 = ("W1", 128, 256)
+    pick(("W1", 192, 256), ("L0", 0, 128), 0, 4, "ofr")
+    front(F1, "tn", K_B, C(12), C(13), 3, O_P1, ("PAR1", 0, 128), ("E1", 0, 128), after1)
+    dma("s", "dp1", [C(13)], [], lambda: T.pa[:, 256:384], lambda: T.col[:, 13:14])
+
+    def gap1(k):
+        t, c = ((0, -2.0 ** 30), (2, 2.0 ** 29), (3, -2.0 ** 23))[k]
+        kfill(K_C, t, c, 0, 64, 0, 64)
+        kfill(K_C, t, c, 64, 128, 64, 128)
+    choose(1, ("E1", 0, 128), K_SB, K(3), K(5), C(14), C(16), C(17), 4, O_L1, gap1)
+    pick(("SN1", 0, 64), ("E1", 0, 128), O_L1, O_L1 + 4)
+    sent += send(1, ("SN1", 0, 64), ("W2", 160, 224), rank ^ PART[1])
+    pick(("W2", 128, 160), ("E1", 0, 128), O_L1 + 2, O_L1 + 4)
+    pick(("W2", 224, 256), ("E1", 0, 128), O_L1, O_L1 + 2)
+
+    row(3, BC)
+    row(4, BD)
+    ts(V("ea", 0, 128), PS(BC, 0, 128), K(0), OP.is_equal)
+    act(V("ebq", 0, 128), IDN, FN.Copy, None, C(15))
+    kquant(K_C)
+    scan(V("sc", 0, 128), V("ea", 0, 128), V("ebq", 0, 128), 0.0, OP.max, OP.max)
+    count("sc", 128, 1.0, None, C(18))
+    ts(sub("ts", 2, 0, 8), K8, C(15), OP.mult, 192.0, OP.mult)
+    copy(V("k2", 0, 2), V("ki", 6, 8))
+    copy(V("k2", 2, 4), V("ki", 0, 2))
+    ts(V("eqi", 64, 128), PS(BD, 0, 64), C(18), OP.is_equal)
+    scan(V("sc", 0, 192), V("eqi", 64, 256), V("eqi", 64, 256), 0.0, OP.max, OP.max)
+    count("sc", 192, 1.0, C(19), C(20))
+    digits("ts", 0, 8, K8, C(19), C(20))
+    fin = carry("ts", 7, 128, BC, O_S1, 8)
+    pick(("PR1", 0, 128), ("PAR1", 0, 128), O_L1, O_L1 + 8)
+    fin()
+
+    def after2(k):
+        if k == 3:
+            quant("WQ", 0, 256, whole("wt", 0, 256))
+        if k == 0:
+            row(5, BC)
+            ts(C(23), C(22), K(0), OP.not_equal)
+        if k == 1:
+            ts(V("eqi", 0, 128), PS(BC, 0, 128), K(0), OP.is_equal)
+            ts(sub("ts", 2, 0, 4), V("k2", 0, 4), C(23), OP.mult, 128.0, OP.mult)
+            scan(V("sc", 0, 256), V("eqi", 0, 256), V("eqi", 0, 256), 0.0, OP.max, OP.max)
+    F2, E2 = ("W2", 128, 256), ("W2", 256, 384)
+    front(F2, "tc", K_C, C(21), C(22), 5, O_P2, ("PAR2", 0, 128), E2, after2)
+    dma("s", "dp2", [C(22)], [], lambda: T.pa[:, 384:448], lambda: T.col[0:64, 22:23])
+
+    count("sc", 256, 1.0, C(24), C(25))
+    opend(("PAR2", 0, 128), K_E1, True)
+    opend(E2, K_E1, False)
+    digits("ts", 0, 4, V("k2", 0, 4), C(24), C(25))
+    fin = carry("ts", 6, 128, BD, O_S2, 4)
+    anew(("W2", 0, 128), True)
+    fin()
+    opend(("PR1", 0, 128), K_E1, True)
+    pick(("W1", 256, 320), ("W2", 0, 384), O_S2, O_S2 + 4)
+    opend(("W1", 192, 320), K_E1, False)
+    anew(("W1", 0, 128), True)
+    pick(("SND", 0, 64), ("W1", 64, 320), O_S1 + 4, O_S1 + 8)
+    sent += send(2, ("SND", 0, 64), ("W0", 384, 448), rank ^ PART[0])
+    pick(("W0", 448, 512), ("W1", 64, 320), O_S1, O_S1 + 4)
+
+    row(2, BD)
+    later(1)
+    pick(("PR0", 0, 128), ("PAR0", 0, 128), O_L0, O_L0 + 8)
+    opend(("PR0", 0, 128), K_E1, True)
+    for b in range(2):
+        ts(sub("ts", 2, 8 * b, 8 * b + 8), K8, C(8 + b), OP.mult, 384.0, OP.mult)
+    digits("ts", 0, 8, K8, C(26), C(27))
+    ts(C(30), C(29), 128.0, OP.is_ge, 128.0, OP.mult)
+    digits("ts", 8, 16, K8, C(28), C(29))
+    ts(sub("ts", 3, 8, 16), K8, C(30), OP.mult)
+    carry("ts", 8, 128, BC, O_S0, 16)()
+    add("v", [V("prow", 0, 128), V("off", O_V, O_V + 8)], [V("par", 0, 256)],
+        lambda: g.vector.tensor_copy(T.par[:, 0:256].indirect(T.off[:, O_V:O_V + 8]), T.prow[:, 0:128]))
+    dma("s", "dp0", [V("par", 0, 256)], [], lambda: T.pa[:, 0:256], lambda: T.par[0:1, 0:256])
+    opend(("W0", 384, 512), K_E1, False)
+    anew(("W0", 0, 128), True)
+    for h in range(2):
+        pick(("FIN", 128 * h, 128 * h + 128), ("W0", 0, 512), O_S0 + 8 * h, O_S0 + 8 * h + 8)
+        for o in range(2):
+            mm(BA + 2 * h + o, ("WQ", 128 * o, 128 * o + 128), ("FIN", 128 * h, 128 * h + 128))
+    dma("s", "doc", [V("qFIN", 0, 256)], [], lambda: T.oc[:, :], lambda: T.qFIN[:, 0:256].bitcast(dt.uint8))
+    for k in range(4):
+        dma("s", "ds%d" % k, [V("sFIN", 0, 256)], [],
+            lambda k=k: T.osc[4 * k:4 * k + 4, :], lambda k=k: T.sFIN[32 * k:32 * k + 4, 0:256])
+    for h in range(2):
+        act(V("ysb", 128 * h, 128 * h + 128), PS(BA + 2 * h, 0, 128), FN.Copy)
+        copy(V("ysb", 256 + 128 * h, 384 + 128 * h), PS(BB + 2 * h, 0, 128))
+    dma("a", "dy0", [V("ysb", 0, 256)], [], lambda: T.y[:, 0:256], lambda: T.ysb[:, 0:256])
+    dma("s", "dy1", [V("ysb", 256, 512)], [], lambda: T.y[:, 256:512], lambda: T.ysb[:, 256:512])
+
+    know = {q: {} for q in queue}
+    for n, o in enumerate(ops):
+        o["clock"] = o["q"] if o["kind"] == "c" else n
+        o["waits"] = []
+        if o["kind"] == "x":
+            o["after"] = {n: n}
+            continue
+        need = {}
+        for m in range(n):
+            e = ops[m]
+            if e["kind"] == "r" or (e["q"] == "p" and o["q"] == "p"):
+                continue
+            hit = any(clash(a, b) for a in o["r"] + o["w"] for b in e["w"]) or any(clash(a, b) for a in o["w"] for b in e["r"])
+            if not hit and e["q"] != o["q"]:
+                hit = any(a[0] == "ps" and clash(a, b) for a in o["r"] for b in e["r"])
+            if hit:
+                need[e["clock"]] = m
+        k = know[o["q"]]
+        for m in sorted(need.values(), reverse=True):
+            e = ops[m]
+            if k.get(e["clock"], -1) < m:
+                o["waits"].append(m)
+                e["inc"] = True
+                for c, i in e["after"].items():
+                    k[c] = max(k.get(c, -1), i)
+        o["after"] = dict(k)
+        o["after"][o["clock"]] = n
+    cnt = {q: 0 for q in queue}
+    for o in ops:
+        if o["kind"] == "c" and o.get("inc"):
+            cnt[o["q"]] += 1
+            o["sem"] = ("c" + o["q"], cnt[o["q"]])
+        if o["kind"] == "d":
+            o["sem"] = (o["sem"], 16)
+    for o in ops:
+        if o["kind"] == "x":
+            continue
+        for m in o["waits"]:
+            queue[o["q"]].wait_ge(T.sem[ops[m]["sem"][0]], ops[m]["sem"][1])
+        ins = o["fn"]()
+        if o["kind"] == "d":
+            ins.then_inc(T.sem[o["sem"][0]], 16)
+        elif o.get("inc"):
+            ins.then_inc(T.sem[o["sem"][0]], 1)
+    for o in ops:
+        if o["kind"] == "d" and not o.get("inc"):
+            queue[o["q"]].wait_ge(T.sem[o["sem"][0]], 16)
+    g.wait_ge(T.sem.snt, sent)

@@ -4,33 +4,36 @@ OP = AluOpType
 FN = ActivationFunctionType
 PART = [1, 4]
 TW = 136
+TY = 168
 BIG = 2.0 ** 90
 TINY = 2.0 ** -100
 LOW = -1.0e29
 
 PAIRS = {"W0": 512, "W1": 320, "W2": 384, "V0": 128, "PAR0": 128, "PR0": 128, "PAR1": 128, "PR1": 128, "PAR2": 128,
-         "E0": 128, "E1": 128, "L0": 128, "SN1": 64, "SND": 64, "FIN": 256, "UQ": 256, "WQ": 256, "KQ": 1920,
-         "CQ": 256, "TQ": 1440}
+         "E0": 128, "E1": 128, "L0": 128, "SN1": 64, "SND": 64, "FIN": 256, "UQ": 256, "WQ": 256, "PARA": 256,
+         "KQ": 2048, "CQ": 256, "TQ": 2112}
 SCRATCH = {}
 for _n, _w in PAIRS.items():
     SCRATCH["q" + _n] = ("sbuf", [128, _w], "float8_e4m3fn_x4")
     SCRATCH["s" + _n] = ("sbuf", [128, _w], "uint8")
-for _n, _w in {"xt": 1024, "wt": 1024, "ut": 16, "ub": 1024, "zb": 520, "eb": 2080, "kt": 3584, "ct": 1024, "tx": 4 * TW,
-               "ty": 4 * TW, "ts": 512, "ht": 512, "tn": 128, "tp": 128, "tc": 128, "df": 256, "junk": 4096}.items():
+for _n, _w in {"xt": 1024, "wt": 1024, "ut": 16, "ub": 1024, "zb": 520, "eb": 2080, "kt": 3584, "k4": 512, "ct": 1024,
+               "tx": 4 * TW, "ty": 4 * TY, "ts": 512, "ht": 512, "tn": 128, "tp": 128, "tc": 128, "df": 256,
+               "junk": 4096}.items():
     SCRATCH[_n] = ("sbuf", [128, _w], "bfloat16")
-for _n, _w in {"zf": 256, "idn": 128, "ki": TW, "k2": 8, "ka": 8, "tmp": 320, "xs": 320, "rr": 256, "zs": 256, "gs": 128, "gd": 128,
-               "gm": 256, "sc": 256, "fl": 256, "eqi": 256, "ea": 128, "ebq": 128, "col": 48, "cst": 8, "par": 256,
-               "prow": 128, "ysb": 512, "m16": 128}.items():
+for _n, _w in {"zf": 256, "idn": 128, "ki": TY, "kb": 32, "g0": 256, "g1": 256, "gm1": 256, "sc1": 256, "sc2": 256,
+               "pall": 256, "dv": 512, "dh": 512, "m4": 128, "bm": 128, "k2": 8, "ka": 8, "tmp": 320, "xs": 320,
+               "rr": 256, "gs": 128, "gd": 128, "gm": 256, "sc": 256, "fl": 256, "eqi": 256, "ea": 128, "ebq": 128,
+               "col": 48, "cst": 8, "par": 256, "prow": 128, "ysb": 512, "m16": 128}.items():
     SCRATCH[_n] = ("sbuf", [128, _w], "float32")
-SCRATCH["mi"] = ("sbuf", [128, 128], "int32")
-SCRATCH["mj"] = ("sbuf", [128, 128], "int32")
-SCRATCH["off"] = ("sbuf", [128, 96], "uint16")
+for _n in ("mi", "mj", "mk", "ml"):
+    SCRATCH[_n] = ("sbuf", [128, 136], "int32")
+SCRATCH["off"] = ("sbuf", [128, 192], "uint16")
 SCRATCH["ofr"] = ("sbuf", [128, 8], "uint16")
 SCRATCH["ps"] = ("psum", [128, 4096], "float32")
 DMAS = ["dx0", "dx1", "du", "dw", "dp0", "dp1", "dp2", "doc", "ds0", "ds1", "ds2", "ds3", "dy0", "dy1"]
 SEMAPHORES = ["cv", "ca", "cp", "cg", "arr0", "arr1", "arr2", "arr3", "snt"] + DMAS
 
-K_A, K_16, K_SA, K_R, K_B, K_SB, K_C, K_E1, K_EH = 0, 1, 2, 3, 4, 5, 6, 7, 11
+K_A, K_16, K_SA, K_R, K_B, K_SB, K_C, K_E1, K_EH, K_4 = 0, 1, 2, 3, 4, 5, 6, 7, 11, 15
 BA, BB, BC, BD = 4, 5, 6, 7
 
 
@@ -118,7 +121,7 @@ def rank_program(g, core, T, topo):
             add("g", reads + [turn_], [o], fn)
 
     def iota(o, pat, base, cm):
-        if o[0] == "mi":
+        if o[0] in ("mi", "mk"):
             pool([], o, lambda: g.iota(ap(o), pat, base, cm))
         else:
             pool([], o, lambda: g.iota(ap(o), pat, base, cm, allow_small_or_imprecise_dtypes=True))
@@ -197,6 +200,8 @@ def rank_program(g, core, T, topo):
     def kquant(slot):
         if slot < K_E1:
             quant("KQ", 128 * slot, 128 * slot + 128, whole("kt", 128 * slot, 128 * slot + 128))
+        elif slot == K_4:
+            quant("KQ", 128 * slot, 128 * slot + 128, whole("k4", 0, 128))
         else:
             h, b = divmod(slot - K_E1, 4)
             at = 520 * (2 * h + b % 2) + (2 - b // 2 * 2)
@@ -212,15 +217,19 @@ def rank_program(g, core, T, topo):
         act(sub(tile, 0, c0, c1), V("zf", 0, c1 - c0), FN.Identity, hi)
 
     def carry(tile, slot, n, bank, o0, k):
-        quant("TQ", 160 * slot, 160 * slot + n, whole(tile, 0, n))
-        mm(bank, kq(K_16), ("TQ", 160 * slot, 160 * slot + 128))
+        quant("TQ", 192 * slot, 192 * slot + n, whole(tile, 0, n))
+        mm(bank, kq(K_16), ("TQ", 192 * slot, 192 * slot + 128))
 
         def fin():
             copy(V("off", o0, o0 + k), PS(bank, 0, k))
         return fin
 
     def row(slot, bank):
-        mm(bank, kq(K_R), ("TQ", 160 * slot + 8, 160 * slot + TW))
+        mm(bank, kq(K_R), ("TQ", 192 * slot + 8, 192 * slot + TW))
+
+    def rowtile(slot, hi, tot):
+        digits("tx", 8, TW, V("ki", 8, TW), C(hi), C(tot))
+        return lambda: quant("TQ", 192 * slot + 8, 192 * slot + TW, whole("tx", 8, TW))
 
     def opend(src, slot0, start):
         for b in range(4):
@@ -237,8 +246,8 @@ def rank_program(g, core, T, topo):
                 copy(o, i)
         quant(*dst, whole("ht", 0, 128))
 
-    def diag(bank, at):
-        tt(V("tmp", at, at + 128), PS(bank, 0, 128), V("idn", 0, 128), OP.mult)
+    def diag(bank, at, c0=0):
+        tt(V("tmp", at, at + 128), PS(bank, c0, c0 + 128), V("idn", 0, 128), OP.mult)
         scan(V("xs", at, at + 160), V("tmp", at, at + 160), V("tmp", at, at + 160), 0.0, OP.max, OP.max)
 
     def turns(at, to):
@@ -252,7 +261,7 @@ def rank_program(g, core, T, topo):
     KI = V("ki", 0, TW)
     K8 = V("ki", 0, 8)
     IDN = V("idn", 0, 128)
-    O_V, O_P0, O_L0, O_P1, O_L1, O_P2, O_S2, O_S1, O_S0 = 0, 8, 16, 24, 32, 40, 48, 56, 64
+    O_V, O_PA, O_L0, O_P1, O_L1, O_P2, O_S2, O_S1, O_S0, O_4 = 112, 96, 16, 24, 32, 40, 48, 56, 64, 128
     for h in range(2):
         dma("s", "dx%d" % h, [], [V("xt", 512 * h, 512 * h + 512)],
             lambda h=h: T.xt[:, 512 * h:512 * h + 512], lambda h=h: T.x[:, 512 * h:512 * h + 512])
@@ -272,13 +281,14 @@ def rank_program(g, core, T, topo):
     for j, (at, c) in enumerate(((2, 1.0), (3, 1.0), (2, -0.5), (3, -0.5))):
         sel(V("eb", 520 * j, 520 * j + 520), V("zb", 0, 520), [[-1, 520]], OP.not_equal, c, at, 4)
     sel(V("tp", 0, 128), V("zb", 0, 128), [[-1, 128]], OP.is_ge, TINY, 0, 1)
+    iota(V("mk", 0, 128), [[0, 8], [-1, 4], [0, 4]], 4, 1)
+    iota(V("mk", 128, 129), [[0, 1]], 0, 1)
+    sel(V("kb", 0, 32), V("zf", 0, 32), [[4, 32]], OP.is_gt, 0.0625, 0, -1)
+    sel(V("ki", TW, TY), V("kb", 0, 32), [[4, 32]], OP.is_ge, 0.0, 3, -1)
     for h in range(2):
         iota(K(4, 64 * h, 64 * h + 64), [[0, 1]], -1, -1)
     for h in range(4):
         iota(K(5, 32 * h, 32 * h + 32), [[0, 1]], -1, -1)
-    iota(V("par", 0, 256), [[1, 256]], 0, 0)
-    sel(V("tc", 0, 128, 1, 0, 64), V("tn", 0, 128, 1, 0, 64), [[-1, 128]], OP.is_gt, -BIG, 64, 0)
-    sel(V("tc", 0, 128, 1, 64, 128), V("tn", 0, 128, 1, 64, 128), [[1, 128]], OP.is_gt, -BIG, -63, 0)
 
     memset(V("tmp", 128, 160), 0.0)
     memset(V("tmp", 288, 320), 0.0)
@@ -286,7 +296,7 @@ def rank_program(g, core, T, topo):
     memset(sub("ct", 3, 0, 256), 1.0)
     for t, c in enumerate((-2.0 ** 30, -2.0 ** 30, 2.0 ** 30, -2.0 ** 22)):
         kfill(K_A, t, c)
-    memset(whole("tx", 0, TW), 0.0)
+    memset(whole("ts", 0, 128), 0.0)
     ts(V("mj", 0, 128), V("mi", 0, 128), 15, OP.bitwise_and)
     kquant(K_A)
     ts(V("m16", 0, 128), V("mj", 0, 128), 0.0, OP.is_equal, 16.0, OP.mult)
@@ -312,59 +322,73 @@ def rank_program(g, core, T, topo):
         act(sub("kt", t, 128 * K_16, 128 * K_16 + 128), V("m16", 0, 128), FN.Copy)
     ubuild(0)
 
-    def gram0(h):
-        quant("W0", 128 + 128 * h, 256 + 128 * h, whole("xt", 128 * h, 128 * h + 128))
-        mm(BA + h, ("W0", 128 + 128 * h, 256 + 128 * h), ("W0", 128 + 128 * h, 256 + 128 * h))
+    Q0, QA, QB = ("W0", 128, 384), ("W0", 128, 256), ("W0", 256, 384)
     d0, d1 = V("xs", 128, 129), V("xs", 288, 289)
-    gram0(0)
-    diag(BA, 0)
-    gram0(1)
+    quant(*QA, whole("xt", 0, 128))
+    mm(BC, QA, QA)
+    diag(BC, 0)
+    quant(*QB, whole("xt", 128, 256))
+    mm(BB, QB, Q0)
+    mm(BA, QA, QB)
+    act(V("g0", 0, 128), PS(BC, 0, 128), FN.Copy, None, 2.0 ** -40)
     turns(0, 0)
     for b in (1, 2, 3):
         act(V("rr", 0, 128, 1, 32 * b, 32 * b + 32), V("rr", 0, 128, 1, 0, 32), FN.Copy)
     act(V("df", 0, 128), V("rr", 0, 128), FN.Identity, d0, -1.0)
-    diag(BB, 160)
+    diag(BB, 160, 128)
     turns(160, 128)
-    for b in (1, 2, 3):
-        act(V("rr", 128, 256, 1, 32 * b, 32 * b + 32), V("rr", 128, 256, 1, 0, 32), FN.Copy)
-    act(V("df", 128, 256), V("rr", 128, 256), FN.Identity, d1, -1.0)
+    for b in range(4):
+        act(V("df", 128, 256, 1, 32 * b, 32 * b + 32), V("rr", 128, 256, 1, 0, 32), FN.Identity,
+            V("xs", 288, 289, 1, 32 * b, 32 * b + 32), -1.0)
     ts(sub("ct", 1, 0, 128), V("rr", 0, 128), d1, OP.is_lt)
+    for b in (1, 2, 3):
+        copy(V("rr", 128, 256, 1, 32 * b, 32 * b + 32), V("rr", 128, 256, 1, 0, 32))
     tt(sub("ct", 0, 0, 128), V("df", 0, 128), V("tn", 0, 128), OP.is_gt)
     ts(sub("ct", 0, 128, 256), V("rr", 128, 256), d0, OP.is_le)
     tt(sub("ct", 1, 128, 256), V("df", 128, 256), V("tn", 0, 128), OP.is_gt)
-    quant("CQ", 0, 256, whole("ct", 0, 256))
-    mm(BA, kq(K_A), ("CQ", 0, 256))
-    kquant(K_16)
-    ts(C(0), K(0), -1.0, OP.mult, -1.0, OP.add)
-    ts(V("fl", 0, 256), PS(BA, 0, 256), 0.0, OP.is_lt)
-    scan(V("sc", 0, 256), V("fl", 0, 256), V("zf", 0, 256), C(0), OP.add, OP.min)
-    act(V("zs", 0, 256), PS(BA, 0, 256), FN.Copy, None, 2.0 ** 40)
-    count("sc", 256, None, C(1), C(2))
-    for s in range(K_E1, K_E1 + 2):
-        kquant(s)
-    digits("tx", 0, TW, KI, C(1), C(2))
-    fin = carry("tx", 0, TW, BB, O_V, 8)
-    kquant(K_E1 + 2)
-    fin()
-    Q0 = ("W0", 128, 384)
-    pick(("V0", 0, 128), Q0, O_V, O_V + 8)
-    mm(BA, ("V0", 0, 128), Q0)
+    act(V("g0", 128, 256), PS(BA, 0, 128), FN.Copy, None, 2.0 ** -40)
+    act(V("g1", 0, 256), PS(BB, 0, 256), FN.Copy, None, 2.0 ** -40)
     ubuild(1)
-    kquant(K_E1 + 3)
-    opend(("V0", 0, 128), K_E1, True)
-    tt(V("gm", 0, 256), PS(BA, 0, 256), V("zs", 0, 256), OP.min)
-    scan(V("sc", 0, 256), V("gm", 0, 256), V("gm", 0, 256), LOW, OP.max, OP.max)
-    count("sc", 256, V("sc", 255, 256), C(3), C(4))
-    for s in range(K_EH, K_EH + 3):
-        kquant(s)
-    digits("tx", 0, TW, KI, C(3), C(4))
-    fin = carry("tx", 1, TW, BB, O_P0, 8)
-    kquant(K_EH + 3)
+    kquant(K_16)
+    quant("CQ", 0, 256, whole("ct", 0, 256))
+    mm(BD, kq(K_A), ("CQ", 0, 256))
+    ts(C(0), K(0), -1.0, OP.mult, -1.0, OP.add)
+    kquant(K_E1)
+    kquant(K_E1 + 1)
+    ts(V("fl", 0, 256), PS(BD, 0, 256), 0.0, OP.is_lt)
+    tt(V("gm", 0, 256), PS(BD, 0, 256), V("g0", 0, 256), OP.min)
+    scan(V("sc", 0, 256), V("fl", 0, 256), V("zf", 0, 256), C(0), OP.add, OP.min)
+    tt(V("gm1", 0, 256), PS(BD, 0, 256), V("g1", 0, 256), OP.min)
+    scan(V("sc1", 0, 256), V("gm", 0, 256), V("gm", 0, 256), LOW, OP.max, OP.max)
+    scan(V("sc2", 0, 256), V("gm1", 0, 256), V("gm1", 0, 256), LOW, OP.max, OP.max)
+    count("sc", 256, None, C(1), C(2))
+    count("sc1", 256, V("sc1", 255, 256), C(3), C(4))
+    count("sc2", 256, V("sc2", 255, 256), C(32), C(33))
+    kquant(K_E1 + 2)
+    ts(V("ml", 0, 129), V("mk", 0, 129), 3, OP.bitwise_and)
+    for c0, hi, tot in ((16, 1, 2), (0, 3, 4), (8, 32, 33)):
+        if c0 == 8:
+            kquant(K_E1 + 3)
+            digits("ts", c0, c0 + 8, K8, C(hi), C(tot))
+        else:
+            ts(sub("ts", 1, c0, c0 + 8), K8, C(tot), OP.mult, C(hi), OP.subtract)
+            ts(sub("ts", 0, c0, c0 + 8), V("zf", 0, 8), C(hi), OP.add)
+    kquant(K_EH)
+    fin = carry("ts", 10, 128, BA, O_PA, 24)
+    kquant(K_EH + 1)
+    kquant(K_EH + 2)
+    ts(V("m4", 0, 128), V("ml", 0, 128), 0.0, OP.is_equal, 64.0, OP.mult)
+    copy(K(6), V("ml", 128, 129))
     fin()
-    pick(("PAR0", 0, 128), Q0, O_P0, O_P0 + 8)
+    kquant(K_EH + 3)
+    pick(("PARA", 0, 256), Q0, O_PA, O_PA + 16)
+    pick(("V0", 0, 128), Q0, O_V, O_V + 8)
+    pick(("PAR0", 0, 128), ("PARA", 0, 256), O_V, O_V + 8)
+    opend(("V0", 0, 128), K_E1, True)
     opend(("PAR0", 0, 128), K_EH, False)
     quant("UQ", 0, 128, whole("ub", 0, 128))
     kquant(K_SA)
+    memset(whole("tx", 0, TW), 0.0)
     anew(("E0", 0, 128), False)
     sent = send(0, ("E0", 0, 128), ("L0", 0, 128), rank ^ PART[0])
 
@@ -377,53 +401,75 @@ def rank_program(g, core, T, topo):
             ts(V("df", 0, 128), PS(BC, 0, 128), PS(BD, 0, 1), OP.subtract)
         else:
             ts(V("df", 0, 128), PS(BC, 0, 128), PS(BD, 0, 1), OP.subtract, mask, OP.add)
+        gap(3)
         tt(sub("ct", 0, 128, 256), V("df", 0, 128), V("tp", 0, 128), OP.is_lt)
         quant("CQ", 128, 256, whole("ct", 128, 256))
         mm(BA, kq(kw), ("CQ", 128, 256))
         gap(1)
         ts(V("fl", 0, 128), PS(BA, 0, 128), thr, OP.is_ge)
+        gap(4)
         scan(V("sc", 0, 128), V("fl", 0, 128), V("zf", 0, 128), start, OP.add, OP.min)
         count("sc", 128, None, hi, tot)
         gap(2)
         digits("tx", 0, TW, KI, hi, tot)
         carry("tx", slot, TW, BB, o0, 8)()
 
+    pend = []
+
     def gap0(k):
         if k == 0:
+            pend.append(rowtile(1, 3, 4))
             kquant(K_R)
         if k == 1:
-            memset(whole("kt", 128 * K_C, 128 * K_C + 128), 0.0)
+            pend.append(rowtile(9, 32, 33))
+            kquant(K_B)
+            for t in range(4):
+                act(sub("k4", t, 0, 128), V("m4" if t < 2 else "zf", 0, 128), FN.Copy)
         if k == 2:
-            memset(whole("ty", 0, TW), 0.0)
+            memset(whole("ty", 0, TY), 0.0)
+        if k > 2:
+            pend.pop()()
     choose(0, ("E0", 0, 128), K_SA, K(2), K(4), None, C(5), C(6), 2, O_L0, gap0)
     sent += send_list(3, V("off", O_L0, O_L0 + 4), V("ofr", 0, 4), rank ^ PART[0])
+    sel(V("bm", 0, 128, 1, 0, 64), V("zf", 0, 128, 1, 0, 64), [[1, 128]], OP.is_gt, 1.0, -63, 0)
+    sel(V("bm", 0, 128, 1, 64, 128), V("zf", 0, 128, 1, 64, 128), [[-1, 128]], OP.is_gt, 1.0, 64, 0)
+    iota(V("par", 0, 256), [[1, 256]], 0, 0)
+    sel(V("tc", 0, 128, 1, 0, 64), V("tn", 0, 128, 1, 0, 64), [[-1, 128]], OP.is_gt, -BIG, 64, 0)
+    sel(V("tc", 0, 128, 1, 64, 128), V("tn", 0, 128, 1, 64, 128), [[1, 128]], OP.is_gt, -BIG, -63, 0)
     pick(("W1", 128, 192), ("E0", 0, 128), O_L0 + 4, O_L0 + 8)
 
-    def later(b):
-        ts(V("eqi", 0, 128), PS(BD, 0, 128), C(10 + b), OP.is_equal)
-        scan(V("sc", 0, 256), V("eqi", 0, 256), V("eqi", 0, 256), 0.0, OP.max, OP.max)
-        count("sc", 256, 1.0, C(26 + 2 * b), C(27 + 2 * b))
-
     row(1, BC)
+    row(9, BA)
+    fin = rowtile(0, 1, 2)
+    act(V("pall", 0, 128), PS(BC, 0, 128), FN.Copy)
+    act(V("pall", 128, 256), PS(BA, 0, 128), FN.Copy)
+    fin()
     row(0, BD)
+    add("a", [V("pall", 0, 256), V("off", O_V, O_V + 8)], [V("prow", 0, 128)],
+        lambda: g.scalar.activation(T.prow[:, 0:128], T.pall[:, 0:256].indirect(T.off[:, O_V:O_V + 8]), FN.Copy))
     act(sub("ty", 2, 8, TW), IDN, FN.Copy, None, 16.0)
     for b in range(2):
-        ts(V("ea", 0, 128), PS(BC, 0, 128), K(b), OP.is_equal)
-        ts(V("ebq", 0, 128), PS(BD, 0, 128), K(b), OP.is_equal)
-        if b == 0:
-            kquant(K_B)
-        else:
-            kquant(K_SB)
-        scan(V("sc", 0, 128), V("ea", 0, 128), V("ebq", 0, 128), 0.0, OP.max, OP.max)
-        act(V("junk", 0, 128), V("ebq", 0, 128), FN.Copy, None, None, C(8 + b))
-        count("sc", 128, 1.0, None, C(10 + b))
-    act(V("prow", 0, 128), PS(BC, 0, 128), FN.Copy)
+        ts(V(("ebq", "fl")[b], 0, 128), PS(BD, 0, 128), K(b), OP.is_equal)
+        ts(V(("ea", "gm1")[b], 0, 128), V("prow", 0, 128), K(b), OP.is_equal)
+    for b in range(2):
+        act(V("junk", 0, 128), V(("ebq", "fl")[b], 0, 128), FN.Copy, None, None, C(8 + b))
+    for b in range(2):
+        scan(V(("sc1", "sc2")[b], 0, 128), V(("ea", "gm1")[b], 0, 128), V(("ebq", "fl")[b], 0, 128), 0.0, OP.max, OP.max)
     row(2, BD)
-    later(0)
 
-    def front(F, tri, kw, hi, tot, slot, o0, PAR, E, after):
+    def later(b, k):
+        r = ("sc1", "sc2")[b]
+        if k == 0:
+            ts(V("eqi", 0, 128), PS(BD, 0, 128), C(10 + b), OP.is_equal)
+        if k == 1:
+            scan(V(r, 0, 256), V("eqi", 0, 256), V("eqi", 0, 256), 0.0, OP.max, OP.max)
+        if k == 2:
+            count(r, 256, 1.0, C(26 + 2 * b), C(27 + 2 * b))
+
+    def front(F, tri, kw, hi, tot, slot, o0, o4c, E, after):
         mm(BA, F, F)
-        opend(F, K_E1, True)
+        for b in range(4):
+            mm(b, kq(K_E1 + b), F)
         diag(BA, 0)
         act(V("gs", 0, 128), PS(BA, 0, 128), FN.Copy, None, 2.0 ** -40)
         sel(V("gd", 0, 128), V("gs", 0, 128), [[-1, 128]], OP.not_equal, 3.0 * 2.0 ** 27, 0, 1)
@@ -435,6 +481,9 @@ def rank_program(g, core, T, topo):
             else:
                 ts(o, i, d, OP.subtract, -1.0, OP.mult)
         tt(sub("ct", 0, 0, 128), V("df", 0, 128), V(tri, 0, 128), OP.is_gt)
+        for b in range(4):
+            act(sub("dv", b, 0, 128), PS(b, 0, 128), FN.Copy)
+            act(sub("dh", b, 0, 128), PS(b, 0, 128), FN.Copy, None, -0.5)
         quant("CQ", 0, 128, whole("ct", 0, 128))
         mm(BB, kq(kw), ("CQ", 0, 128))
         after(2)
@@ -442,57 +491,76 @@ def rank_program(g, core, T, topo):
         scan(V("sc", 0, 128), V("gm", 0, 128), V("gm", 0, 128), LOW, OP.max, OP.max)
         count("sc", 128, V("sc", 127, 128), hi, tot)
         after(3)
-        digits("ty", 0, TW, KI, hi, tot)
-        fin = carry("ty", slot, TW, BA, o0, 8)
+        digits("ty", 0, TY, V("ki", 0, TY), hi, tot)
+        quant("TQ", 192 * slot, 192 * slot + TY, whole("ty", 0, TY))
+        mm(BB, kq(K_4), ("TQ", 192 * slot + 40, 192 * slot + TY))
+        mm(BA, kq(K_16), ("TQ", 192 * slot, 192 * slot + 128))
         after(0)
-        fin()
-        pick(PAR, F, o0, o0 + 8)
-        opend(PAR, K_EH, False)
+        o4 = V("off", o4c, o4c + 32)
+        ts(o4, PS(BB, 96, 128), K(6), OP.add)
+        copy(V("off", o0, o0 + 8), PS(BA, 0, 8))
+        after(4)
+        add("v", [V("dh", 0, 512), V("dv", 0, 512), o4], [V("ht", 0, 512)],
+            lambda: g.vector.tensor_tensor(T.ht[:, 0:512], T.dh[:, 0:512].indirect(ap(o4)), T.dv[:, 0:512], OP.add))
         after(1)
-        anew(E, False)
+        quant(*E, whole("ht", 0, 128))
 
     def after1(k):
         if k == 2:
             quant("UQ", 128, 256, whole("ub", 128, 256))
+            kquant(K_4)
+            later(0, 0)
         if k == 3:
-            memset(whole("ts", 0, 128), 0.0)
+            later(0, 1)
+            kquant(K_SB)
         if k == 0:
             ts(C(14), C(13), K(0), OP.is_equal, BIG, OP.mult)
+            later(1, 0)
+            later(0, 2)
+        if k == 4:
+            later(1, 1)
+            later(1, 2)
+            for t, c in enumerate((-2.0 ** 30, 0.0, 2.0 ** 29, -2.0 ** 23)):
+                act(sub("kt", t, 128 * K_C, 128 * K_C + 128), V("bm", 0, 128), FN.Copy, None, c)
         if k == 1:
             ts(sub("ct", 1, 128, 256), IDN, C(14), OP.mult, 1.0 / BIG, OP.mult)
             ts(C(15), C(13), K(0), OP.not_equal)
     F1 = ("W1", 128, 256)
     pick(("W1", 192, 256), ("L0", 0, 128), 0, 4, "ofr")
-    front(F1, "tn", K_B, C(12), C(13), 3, O_P1, ("PAR1", 0, 128), ("E1", 0, 128), after1)
+    for b in range(2):
+        count(("sc1", "sc2")[b], 128, 1.0, None, C(10 + b))
+    front(F1, "tn", K_B, C(12), C(13), 3, O_P1, O_4, ("E1", 0, 128), after1)
     dma("s", "dp1", [C(13)], [], lambda: T.pa[:, 256:384], lambda: T.col[:, 13:14])
 
     def gap1(k):
-        t, c = ((0, -2.0 ** 30), (2, 2.0 ** 29), (3, -2.0 ** 23))[k]
-        kfill(K_C, t, c, 0, 64, 0, 64)
-        kfill(K_C, t, c, 64, 128, 64, 128)
+        if k == 0:
+            row(3, BB)
+            act(V("ebq", 0, 128), IDN, FN.Copy, None, C(15))
+            pick(("PAR1", 0, 128), F1, O_P1, O_P1 + 8)
+        if k == 3:
+            ts(V("ea", 0, 128), PS(BB, 0, 128), K(0), OP.is_equal)
+        if k == 4:
+            scan(V("sc1", 0, 128), V("ea", 0, 128), V("ebq", 0, 128), 0.0, OP.max, OP.max)
+            count("sc1", 128, 1.0, None, C(18))
+        if k == 1:
+            kquant(K_C)
+            copy(V("k2", 0, 2), V("ki", 6, 8))
+            copy(V("k2", 2, 4), V("ki", 0, 2))
+        if k == 2:
+            ts(sub("ts", 2, 0, 8), K8, C(15), OP.mult, 192.0, OP.mult)
     choose(1, ("E1", 0, 128), K_SB, K(3), K(5), C(14), C(16), C(17), 4, O_L1, gap1)
     pick(("SN1", 0, 64), ("E1", 0, 128), O_L1, O_L1 + 4)
     sent += send(1, ("SN1", 0, 64), ("W2", 160, 224), rank ^ PART[1])
     pick(("W2", 128, 160), ("E1", 0, 128), O_L1 + 2, O_L1 + 4)
     pick(("W2", 224, 256), ("E1", 0, 128), O_L1, O_L1 + 2)
 
-    row(3, BC)
     row(4, BD)
-    ts(V("ea", 0, 128), PS(BC, 0, 128), K(0), OP.is_equal)
-    act(V("ebq", 0, 128), IDN, FN.Copy, None, C(15))
-    kquant(K_C)
-    scan(V("sc", 0, 128), V("ea", 0, 128), V("ebq", 0, 128), 0.0, OP.max, OP.max)
-    count("sc", 128, 1.0, None, C(18))
-    ts(sub("ts", 2, 0, 8), K8, C(15), OP.mult, 192.0, OP.mult)
-    copy(V("k2", 0, 2), V("ki", 6, 8))
-    copy(V("k2", 2, 4), V("ki", 0, 2))
+    pick(("PR1", 0, 128), ("PAR1", 0, 128), O_L1, O_L1 + 8)
     ts(V("eqi", 64, 128), PS(BD, 0, 64), C(18), OP.is_equal)
     scan(V("sc", 0, 192), V("eqi", 64, 256), V("eqi", 64, 256), 0.0, OP.max, OP.max)
     count("sc", 192, 1.0, C(19), C(20))
     digits("ts", 0, 8, K8, C(19), C(20))
-    fin = carry("ts", 7, 128, BC, O_S1, 8)
-    pick(("PR1", 0, 128), ("PAR1", 0, 128), O_L1, O_L1 + 8)
-    fin()
+    carry("ts", 7, 128, BC, O_S1, 8)()
 
     def after2(k):
         if k == 3:
@@ -500,12 +568,14 @@ def rank_program(g, core, T, topo):
         if k == 0:
             row(5, BC)
             ts(C(23), C(22), K(0), OP.not_equal)
-        if k == 1:
-            ts(V("eqi", 0, 128), PS(BC, 0, 128), K(0), OP.is_equal)
+        if k == 4:
             ts(sub("ts", 2, 0, 4), V("k2", 0, 4), C(23), OP.mult, 128.0, OP.mult)
+            ts(V("eqi", 0, 128), PS(BC, 0, 128), K(0), OP.is_equal)
+        if k == 1:
             scan(V("sc", 0, 256), V("eqi", 0, 256), V("eqi", 0, 256), 0.0, OP.max, OP.max)
+            pick(("PAR2", 0, 128), ("W2", 128, 256), O_P2, O_P2 + 8)
     F2, E2 = ("W2", 128, 256), ("W2", 256, 384)
-    front(F2, "tc", K_C, C(21), C(22), 5, O_P2, ("PAR2", 0, 128), E2, after2)
+    front(F2, "tc", K_C, C(21), C(22), 5, O_P2, O_4 + 32, E2, after2)
     dma("s", "dp2", [C(22)], [], lambda: T.pa[:, 384:448], lambda: T.col[0:64, 22:23])
 
     count("sc", 256, 1.0, C(24), C(25))
@@ -523,8 +593,6 @@ def rank_program(g, core, T, topo):
     sent += send(2, ("SND", 0, 64), ("W0", 384, 448), rank ^ PART[0])
     pick(("W0", 448, 512), ("W1", 64, 320), O_S1, O_S1 + 4)
 
-    row(2, BD)
-    later(1)
     pick(("PR0", 0, 128), ("PAR0", 0, 128), O_L0, O_L0 + 8)
     opend(("PR0", 0, 128), K_E1, True)
     for b in range(2):

@@ -17,20 +17,19 @@ for _n, _w in PAIRS.items():
     SCRATCH["q" + _n] = ("sbuf", [128, _w], "float8_e4m3fn_x4")
     SCRATCH["s" + _n] = ("sbuf", [128, _w], "uint8")
 for _n, _w in {"xt": 1024, "wt": 1024, "ut": 16, "ub": 1024, "zb": 520, "eb": 2080, "kt": 3584, "k4": 512, "ct": 1024,
-               "tx": 4 * TW, "ty": 4 * TY, "ts": 512, "ht": 512, "tn": 128, "tp": 128, "tc": 128, "df": 256,
-               "junk": 4096}.items():
+               "tx": 4 * TW, "ty": 4 * TY, "ts": 512, "ht": 512, "tn": 128, "tp": 128, "df": 256, "junk": 4096}.items():
     SCRATCH[_n] = ("sbuf", [128, _w], "bfloat16")
 for _n, _w in {"zf": 256, "idn": 128, "ki": TY, "kb": 32, "g0": 256, "g1": 256, "gm1": 256, "sc1": 256, "sc2": 256,
-               "pall": 256, "dv": 512, "dh": 512, "m4": 128, "bm": 128, "k2": 8, "ka": 8, "tmp": 320, "xs": 320,
-               "rr": 256, "gs": 128, "gd": 128, "gm": 256, "sc": 256, "fl": 256, "eqi": 256, "ea": 128, "ebq": 128,
-               "col": 48, "cst": 8, "par": 256, "prow": 128, "ysb": 512, "m16": 128}.items():
+               "pall": 256, "dv": 512, "dh": 512, "m4": 128, "r1": 128, "xc": 32, "bm": 128, "k2": 8, "ka": 8,
+               "tmp": 320, "xs": 320, "rr": 256, "gs": 128, "gd": 128, "gm": 256, "sc": 256, "fl": 256, "eqi": 256,
+               "ea": 128, "ebq": 128, "col": 48, "cst": 8, "par": 256, "prow": 128, "ysb": 512, "m16": 128}.items():
     SCRATCH[_n] = ("sbuf", [128, _w], "float32")
 for _n in ("mi", "mj", "mk", "ml"):
     SCRATCH[_n] = ("sbuf", [128, 136], "int32")
 SCRATCH["off"] = ("sbuf", [128, 192], "uint16")
 SCRATCH["ofr"] = ("sbuf", [128, 8], "uint16")
 SCRATCH["ps"] = ("psum", [128, 4096], "float32")
-DMAS = ["dx0", "dx1", "du", "dw", "dp0", "dp1", "dp2", "doc", "ds0", "ds1", "ds2", "ds3", "dy0", "dy1"]
+DMAS = ["dx0", "dx1", "du", "dw", "dp0", "dp1", "dp2", "doc", "ds0", "ds1", "ds2", "ds3", "dy0"]
 SEMAPHORES = ["cv", "ca", "cp", "cg", "arr0", "arr1", "arr2", "arr3", "snt"] + DMAS
 
 K_A, K_16, K_SA, K_R, K_B, K_SB, K_C, K_E1, K_EH, K_4 = 0, 1, 2, 3, 4, 5, 6, 7, 11, 15
@@ -113,6 +112,9 @@ def rank_program(g, core, T, topo):
         add("a", views(i, bias, scale), views(o, acc),
             lambda: g.scalar.activation(ap(o), ap(i), fn, **{k: ap(x) for k, x in kw.items()}))
 
+    def grab(o, win, of):
+        add("a", [win, of], [o], lambda: g.scalar.activation(ap(o), ap(win).indirect(ap(of)), FN.Copy))
+
     def pool(reads, o, fn):
         turn_ = V("pool", 0, 1)
         if o[2] - o[1] < 128:
@@ -152,7 +154,7 @@ def rank_program(g, core, T, topo):
         of = V(lists, o0, o1)
         add("v", [qw, of], [qd], lambda: g.vector.tensor_copy(
             ap(qd).bitcast(dt.uint32), ap(qw).bitcast(dt.uint32).indirect(ap(of))))
-        add("a", [sw, of], [sd], lambda: g.scalar.activation(ap(sd), ap(sw).indirect(ap(of)), FN.Copy))
+        grab(sd, sw, of)
 
     def dma(q, sem, reads, writes, out, in_):
         add(q, reads, writes, lambda: queue[q].dma_start(out(), in_()), sem, "d")
@@ -246,13 +248,16 @@ def rank_program(g, core, T, topo):
                 copy(o, i)
         quant(*dst, whole("ht", 0, 128))
 
-    def diag(bank, at, c0=0):
-        tt(V("tmp", at, at + 128), PS(bank, c0, c0 + 128), V("idn", 0, 128), OP.mult)
+    def diag(bank, at):
+        tt(V("tmp", at, at + 128), PS(bank, 0, 128), V("idn", 0, 128), OP.mult)
         scan(V("xs", at, at + 160), V("tmp", at, at + 160), V("tmp", at, at + 160), 0.0, OP.max, OP.max)
 
     def turns(at, to):
         for a in range(4):
             turn(V("rr", to + 32 * a, to + 32 * a + 32, 1, 0, 32), V("xs", at + 128, at + 160, 1, 32 * a, 32 * a + 32))
+
+    def upright(a):
+        turn(V("xc", 0, 32, 1, 32 * a, 32 * a + 32), V("r1", 32 * a, 32 * a + 32, 1, 0, 32))
 
     def ubuild(l):
         for t in range(4):
@@ -328,14 +333,15 @@ def rank_program(g, core, T, topo):
     mm(BC, QA, QA)
     diag(BC, 0)
     quant(*QB, whole("xt", 128, 256))
-    mm(BB, QB, Q0)
+    mm(BB, QB, QB)
     mm(BA, QA, QB)
+    mm(0, QB, QA)
     act(V("g0", 0, 128), PS(BC, 0, 128), FN.Copy, None, 2.0 ** -40)
     turns(0, 0)
     for b in (1, 2, 3):
         act(V("rr", 0, 128, 1, 32 * b, 32 * b + 32), V("rr", 0, 128, 1, 0, 32), FN.Copy)
     act(V("df", 0, 128), V("rr", 0, 128), FN.Identity, d0, -1.0)
-    diag(BB, 160, 128)
+    diag(BB, 160)
     turns(160, 128)
     for b in range(4):
         act(V("df", 128, 256, 1, 32 * b, 32 * b + 32), V("rr", 128, 256, 1, 0, 32), FN.Identity,
@@ -347,7 +353,8 @@ def rank_program(g, core, T, topo):
     ts(sub("ct", 0, 128, 256), V("rr", 128, 256), d0, OP.is_le)
     tt(sub("ct", 1, 128, 256), V("df", 128, 256), V("tn", 0, 128), OP.is_gt)
     act(V("g0", 128, 256), PS(BA, 0, 128), FN.Copy, None, 2.0 ** -40)
-    act(V("g1", 0, 256), PS(BB, 0, 256), FN.Copy, None, 2.0 ** -40)
+    act(V("g1", 0, 128), PS(0, 0, 128), FN.Copy, None, 2.0 ** -40)
+    act(V("g1", 128, 256), PS(BB, 0, 128), FN.Copy, None, 2.0 ** -40)
     ubuild(1)
     kquant(K_16)
     quant("CQ", 0, 256, whole("ct", 0, 256))
@@ -426,36 +433,39 @@ def rank_program(g, core, T, topo):
             for t in range(4):
                 act(sub("k4", t, 0, 128), V("m4" if t < 2 else "zf", 0, 128), FN.Copy)
         if k == 2:
+            mm(0, ("E0", 0, 128), ("E0", 0, 128))
+            tt(V("tmp", 0, 128), PS(0, 0, 128), IDN, OP.mult)
             memset(whole("ty", 0, TY), 0.0)
+            scan(V("xs", 0, 160), V("tmp", 0, 160), V("tmp", 0, 160), 0.0, OP.max, OP.max)
         if k > 2:
             pend.pop()()
     choose(0, ("E0", 0, 128), K_SA, K(2), K(4), None, C(5), C(6), 2, O_L0, gap0)
     sent += send_list(3, V("off", O_L0, O_L0 + 4), V("ofr", 0, 4), rank ^ PART[0])
     sel(V("bm", 0, 128, 1, 0, 64), V("zf", 0, 128, 1, 0, 64), [[1, 128]], OP.is_gt, 1.0, -63, 0)
     sel(V("bm", 0, 128, 1, 64, 128), V("zf", 0, 128, 1, 64, 128), [[-1, 128]], OP.is_gt, 1.0, 64, 0)
-    iota(V("par", 0, 256), [[1, 256]], 0, 0)
-    sel(V("tc", 0, 128, 1, 0, 64), V("tn", 0, 128, 1, 0, 64), [[-1, 128]], OP.is_gt, -BIG, 64, 0)
-    sel(V("tc", 0, 128, 1, 64, 128), V("tn", 0, 128, 1, 64, 128), [[1, 128]], OP.is_gt, -BIG, -63, 0)
-    pick(("W1", 128, 192), ("E0", 0, 128), O_L0 + 4, O_L0 + 8)
 
+    mm(1, ("L0", 0, 128), ("L0", 0, 128))
+    turns(0, 0)
+    tt(V("tmp", 160, 288), PS(1, 0, 128), IDN, OP.mult)
+    for b in (1, 2, 3):
+        act(V("rr", 0, 128, 1, 32 * b, 32 * b + 32), V("rr", 0, 128, 1, 0, 32), FN.Copy)
+    pick(("W1", 128, 192), ("E0", 0, 128), O_L0 + 4, O_L0 + 8)
+    scan(V("xs", 160, 320), V("tmp", 160, 320), V("tmp", 160, 320), 0.0, OP.max, OP.max)
+    grab(V("r1", 0, 64), V("rr", 0, 128), V("off", O_L0 + 4, O_L0 + 8))
     row(1, BC)
-    row(9, BA)
-    fin = rowtile(0, 1, 2)
+    row(9, BD)
+    pend.append(rowtile(0, 1, 2))
+    turns(160, 128)
+    copy(V("rr", 128, 256, 1, 32, 64), V("rr", 128, 256, 1, 0, 32))
+    act(V("rr", 128, 256, 1, 64, 96), V("rr", 128, 256, 1, 0, 32), FN.Copy)
+    copy(V("rr", 128, 256, 1, 96, 128), V("rr", 128, 256, 1, 0, 32))
+    upright(0)
+    upright(1)
+    pend.pop()()
     act(V("pall", 0, 128), PS(BC, 0, 128), FN.Copy)
-    act(V("pall", 128, 256), PS(BA, 0, 128), FN.Copy)
-    fin()
+    act(V("pall", 128, 256), PS(BD, 0, 128), FN.Copy)
     row(0, BD)
-    add("a", [V("pall", 0, 256), V("off", O_V, O_V + 8)], [V("prow", 0, 128)],
-        lambda: g.scalar.activation(T.prow[:, 0:128], T.pall[:, 0:256].indirect(T.off[:, O_V:O_V + 8]), FN.Copy))
     act(sub("ty", 2, 8, TW), IDN, FN.Copy, None, 16.0)
-    for b in range(2):
-        ts(V(("ebq", "fl")[b], 0, 128), PS(BD, 0, 128), K(b), OP.is_equal)
-        ts(V(("ea", "gm1")[b], 0, 128), V("prow", 0, 128), K(b), OP.is_equal)
-    for b in range(2):
-        act(V("junk", 0, 128), V(("ebq", "fl")[b], 0, 128), FN.Copy, None, None, C(8 + b))
-    for b in range(2):
-        scan(V(("sc1", "sc2")[b], 0, 128), V(("ea", "gm1")[b], 0, 128), V(("ebq", "fl")[b], 0, 128), 0.0, OP.max, OP.max)
-    row(2, BD)
 
     def later(b, k):
         r = ("sc1", "sc2")[b]
@@ -466,21 +476,29 @@ def rank_program(g, core, T, topo):
         if k == 2:
             count(r, 256, 1.0, C(26 + 2 * b), C(27 + 2 * b))
 
-    def front(F, tri, kw, hi, tot, slot, o0, o4c, E, after):
+    def front(F, l, kw, hi, tot, slot, o0, o4c, E, after):
         mm(BA, F, F)
         for b in range(4):
             mm(b, kq(K_E1 + b), F)
-        diag(BA, 0)
+        if l == 2:
+            diag(BA, 0)
         act(V("gs", 0, 128), PS(BA, 0, 128), FN.Copy, None, 2.0 ** -40)
         sel(V("gd", 0, 128), V("gs", 0, 128), [[-1, 128]], OP.not_equal, 3.0 * 2.0 ** 27, 0, 1)
-        turns(0, 0)
-        for b in (2, 0, 3, 1):
-            o, i, d = V("df", 0, 128, 1, 32 * b, 32 * b + 32), V("rr", 0, 128, 1, 0, 32), V("xs", 128, 129, 1, 32 * b, 32 * b + 32)
-            if b >= 2:
-                act(o, i, FN.Identity, d, -1.0)
-            else:
-                ts(o, i, d, OP.subtract, -1.0, OP.mult)
-        tt(sub("ct", 0, 0, 128), V("df", 0, 128), V(tri, 0, 128), OP.is_gt)
+        if l == 1:
+            upright(2)
+            upright(3)
+            ts(V("df", 0, 128), V("r1", 0, 128), V("xc", 0, 1), OP.subtract, -1.0, OP.mult)
+            tt(sub("ct", 0, 0, 128), V("df", 0, 128), V("tn", 0, 128), OP.is_gt)
+        else:
+            turn(V("xc", 0, 32), V("xs", 128, 160))
+            ts(V("df", 0, 32), V("xc", 0, 32), V("xs", 128, 129), OP.subtract, -1.0, OP.mult)
+            for a in range(4):
+                b = a ^ 1
+                ts(sub("ct", 0, 32 * b, 32 * b + 32, 32 * a, 32 * a + 32), V("xc", 0, 32, 1, 32 * b, 32 * b + 32),
+                   V("xs", 128, 129, 1, 32 * a, 32 * a + 32), OP.is_le if a < b else OP.is_lt)
+            for a in range(4):
+                tt(sub("ct", 0, 32 * a, 32 * a + 32, 32 * a, 32 * a + 32), V("df", 0, 32, 1, 32 * a, 32 * a + 32),
+                   V("tn", 32 * a, 32 * a + 32, 1, 32 * a, 32 * a + 32), OP.is_gt)
         for b in range(4):
             act(sub("dv", b, 0, 128), PS(b, 0, 128), FN.Copy)
             act(sub("dh", b, 0, 128), PS(b, 0, 128), FN.Copy, None, -0.5)
@@ -509,27 +527,30 @@ def rank_program(g, core, T, topo):
         if k == 2:
             quant("UQ", 128, 256, whole("ub", 128, 256))
             kquant(K_4)
-            later(0, 0)
+            grab(V("prow", 0, 128), V("pall", 0, 256), V("off", O_V, O_V + 8))
         if k == 3:
-            later(0, 1)
             kquant(K_SB)
+            for b in range(2):
+                ts(V(("ebq", "fl")[b], 0, 128), PS(BD, 0, 128), K(b), OP.is_equal)
+                ts(V(("ea", "gm1")[b], 0, 128), V("prow", 0, 128), K(b), OP.is_equal)
         if k == 0:
             ts(C(14), C(13), K(0), OP.is_equal, BIG, OP.mult)
-            later(1, 0)
-            later(0, 2)
+            for b in range(2):
+                scan(V(("sc1", "sc2")[b], 0, 128), V(("ea", "gm1")[b], 0, 128), V(("ebq", "fl")[b], 0, 128), 0.0, OP.max, OP.max)
+                act(V("junk", 0, 128), V(("ebq", "fl")[b], 0, 128), FN.Copy, None, None, C(8 + b))
         if k == 4:
-            later(1, 1)
-            later(1, 2)
+            for b in range(2):
+                count(("sc1", "sc2")[b], 128, 1.0, None, C(10 + b))
             for t, c in enumerate((-2.0 ** 30, 0.0, 2.0 ** 29, -2.0 ** 23)):
                 act(sub("kt", t, 128 * K_C, 128 * K_C + 128), V("bm", 0, 128), FN.Copy, None, c)
         if k == 1:
             ts(sub("ct", 1, 128, 256), IDN, C(14), OP.mult, 1.0 / BIG, OP.mult)
             ts(C(15), C(13), K(0), OP.not_equal)
     F1 = ("W1", 128, 256)
+    grab(V("r1", 64, 128), V("rr", 128, 256), V("ofr", 0, 4))
     pick(("W1", 192, 256), ("L0", 0, 128), 0, 4, "ofr")
-    for b in range(2):
-        count(("sc1", "sc2")[b], 128, 1.0, None, C(10 + b))
-    front(F1, "tn", K_B, C(12), C(13), 3, O_P1, O_4, ("E1", 0, 128), after1)
+    front(F1, 1, K_B, C(12), C(13), 3, O_P1, O_4, ("E1", 0, 128), after1)
+    iota(V("par", 0, 256), [[1, 256]], 0, 0)
     dma("s", "dp1", [C(13)], [], lambda: T.pa[:, 256:384], lambda: T.col[:, 13:14])
 
     def gap1(k):
@@ -557,17 +578,28 @@ def rank_program(g, core, T, topo):
     row(4, BD)
     pick(("PR1", 0, 128), ("PAR1", 0, 128), O_L1, O_L1 + 8)
     ts(V("eqi", 64, 128), PS(BD, 0, 64), C(18), OP.is_equal)
+    memset(sub("ct", 0, 64, 128, 0, 64), 1.0)
+    memset(sub("ct", 0, 0, 64, 64, 128), 1.0)
     scan(V("sc", 0, 192), V("eqi", 64, 256), V("eqi", 64, 256), 0.0, OP.max, OP.max)
     count("sc", 192, 1.0, C(19), C(20))
-    digits("ts", 0, 8, K8, C(19), C(20))
-    carry("ts", 7, 128, BC, O_S1, 8)()
+    add("v", [V("prow", 0, 128), V("off", O_V, O_V + 8)], [V("par", 0, 256)],
+        lambda: g.vector.tensor_copy(T.par[:, 0:256].indirect(T.off[:, O_V:O_V + 8]), T.prow[:, 0:128]))
+    dma("s", "dp0", [V("par", 0, 256)], [], lambda: T.pa[:, 0:256], lambda: T.par[0:1, 0:256])
+    row(2, BD)
+    quant("WQ", 0, 256, whole("wt", 0, 256))
 
     def after2(k):
+        if k == 2:
+            digits("ts", 0, 8, K8, C(19), C(20))
+            later(0, 0)
         if k == 3:
-            quant("WQ", 0, 256, whole("wt", 0, 256))
+            pend.append(carry("ts", 7, 128, 0, O_S1, 8))
+            later(0, 1)
         if k == 0:
             row(5, BC)
             ts(C(23), C(22), K(0), OP.not_equal)
+            later(0, 2)
+            pend.pop()()
         if k == 4:
             ts(sub("ts", 2, 0, 4), V("k2", 0, 4), C(23), OP.mult, 128.0, OP.mult)
             ts(V("eqi", 0, 128), PS(BC, 0, 128), K(0), OP.is_equal)
@@ -575,7 +607,7 @@ def rank_program(g, core, T, topo):
             scan(V("sc", 0, 256), V("eqi", 0, 256), V("eqi", 0, 256), 0.0, OP.max, OP.max)
             pick(("PAR2", 0, 128), ("W2", 128, 256), O_P2, O_P2 + 8)
     F2, E2 = ("W2", 128, 256), ("W2", 256, 384)
-    front(F2, "tc", K_C, C(21), C(22), 5, O_P2, O_4 + 32, E2, after2)
+    front(F2, 2, K_C, C(21), C(22), 5, O_P2, O_4 + 32, E2, after2)
     dma("s", "dp2", [C(22)], [], lambda: T.pa[:, 384:448], lambda: T.col[0:64, 22:23])
 
     count("sc", 256, 1.0, C(24), C(25))
@@ -588,11 +620,15 @@ def rank_program(g, core, T, topo):
     opend(("PR1", 0, 128), K_E1, True)
     pick(("W1", 256, 320), ("W2", 0, 384), O_S2, O_S2 + 4)
     opend(("W1", 192, 320), K_E1, False)
+    row(2, BD)
     anew(("W1", 0, 128), True)
+    later(1, 0)
     pick(("SND", 0, 64), ("W1", 64, 320), O_S1 + 4, O_S1 + 8)
     sent += send(2, ("SND", 0, 64), ("W0", 384, 448), rank ^ PART[0])
+    later(1, 1)
     pick(("W0", 448, 512), ("W1", 64, 320), O_S1, O_S1 + 4)
 
+    later(1, 2)
     pick(("PR0", 0, 128), ("PAR0", 0, 128), O_L0, O_L0 + 8)
     opend(("PR0", 0, 128), K_E1, True)
     for b in range(2):
@@ -602,9 +638,6 @@ def rank_program(g, core, T, topo):
     digits("ts", 8, 16, K8, C(28), C(29))
     ts(sub("ts", 3, 8, 16), K8, C(30), OP.mult)
     carry("ts", 8, 128, BC, O_S0, 16)()
-    add("v", [V("prow", 0, 128), V("off", O_V, O_V + 8)], [V("par", 0, 256)],
-        lambda: g.vector.tensor_copy(T.par[:, 0:256].indirect(T.off[:, O_V:O_V + 8]), T.prow[:, 0:128]))
-    dma("s", "dp0", [V("par", 0, 256)], [], lambda: T.pa[:, 0:256], lambda: T.par[0:1, 0:256])
     opend(("W0", 384, 512), K_E1, False)
     anew(("W0", 0, 128), True)
     for h in range(2):
@@ -618,8 +651,7 @@ def rank_program(g, core, T, topo):
     for h in range(2):
         act(V("ysb", 128 * h, 128 * h + 128), PS(BA + 2 * h, 0, 128), FN.Copy)
         copy(V("ysb", 256 + 128 * h, 384 + 128 * h), PS(BB + 2 * h, 0, 128))
-    dma("a", "dy0", [V("ysb", 0, 256)], [], lambda: T.y[:, 0:256], lambda: T.ysb[:, 0:256])
-    dma("s", "dy1", [V("ysb", 256, 512)], [], lambda: T.y[:, 256:512], lambda: T.ysb[:, 256:512])
+    dma("a", "dy0", [V("ysb", 0, 512)], [], lambda: T.y[:, :], lambda: T.ysb[:, :])
 
     know = {q: {} for q in queue}
     for n, o in enumerate(ops):

@@ -10,19 +10,20 @@ TINY = 2.0 ** -100
 LOW = -1.0e29
 
 PAIRS = {"W0": 512, "W1": 320, "W2": 384, "V0": 128, "PAR0": 128, "PR0": 128, "PAR1": 128, "PR1": 128, "PAR2": 128,
-         "E0": 128, "E1": 128, "L0": 128, "SN1": 64, "SND": 64, "FIN": 256, "UQ": 256, "WQ": 256, "PARA": 256,
+         "E0": 128, "E1": 128, "L0": 128, "SN1": 64, "SND": 64, "FIN": 256, "UQ": 512, "WQ": 256, "PARA": 256,
          "KQ": 2048, "CQ": 256, "TQ": 2112}
 SCRATCH = {}
 for _n, _w in PAIRS.items():
     SCRATCH["q" + _n] = ("sbuf", [128, _w], "float8_e4m3fn_x4")
     SCRATCH["s" + _n] = ("sbuf", [128, _w], "uint8")
-for _n, _w in {"xt": 1024, "wt": 1024, "ut": 16, "ub": 1024, "zb": 520, "eb": 2080, "kt": 3584, "k4": 512, "ct": 1024,
-               "tx": 4 * TW, "ty": 4 * TY, "ts": 512, "ht": 512, "tn": 128, "tp": 128, "df": 256, "junk": 4096}.items():
+for _n, _w in {"xt": 1024, "wt": 1024, "ut": 16, "ub": 2048, "zb": 520, "eb": 2080, "kt": 3584, "k4": 512, "ct": 1024,
+               "ty": 4 * TY, "ts": 512, "ht": 512, "tn": 128, "tp": 128, "tq": 128, "df": 256, "junk": 6144}.items():
     SCRATCH[_n] = ("sbuf", [128, _w], "bfloat16")
 for _n, _w in {"zf": 256, "idn": 128, "ki": TY, "kb": 32, "g0": 256, "g1": 256, "gm1": 256, "sc1": 256, "sc2": 256,
                "pall": 256, "dv": 512, "dh": 512, "m4": 128, "r1": 128, "xc": 32, "bm": 128, "k2": 8, "ka": 8,
                "tmp": 320, "xs": 320, "rr": 256, "gs": 128, "gd": 128, "gm": 256, "sc": 256, "fl": 256, "eqi": 256,
-               "ea": 128, "ebq": 128, "col": 48, "cst": 8, "par": 256, "prow": 128, "ysb": 512, "m16": 128}.items():
+               "ea": 128, "ebq": 128, "col": 48, "cst": 8, "par": 256, "prow": 128, "ysb": 512, "m16": 128,
+               "num": 256, "thr": 8, "un": 8, "npr": 128, "lrv": 128, "lr0": 128, "lr1": 64}.items():
     SCRATCH[_n] = ("sbuf", [128, _w], "float32")
 for _n in ("mi", "mj", "mk", "ml"):
     SCRATCH[_n] = ("sbuf", [128, 136], "int32")
@@ -34,6 +35,25 @@ SEMAPHORES = ["cv", "ca", "cp", "cg", "arr0", "arr1", "arr2", "arr3", "snt"] + D
 
 K_A, K_16, K_SA, K_R, K_B, K_SB, K_C, K_E1, K_EH, K_4 = 0, 1, 2, 3, 4, 5, 6, 7, 11, 15
 BA, BB, BC, BD = 4, 5, 6, 7
+
+ISSUE = [
+    0,20,4,7,24,2,29,6,31,25,42,40,12,45,44,30,41,28,27,11,33,10,37,22,5,35,43,36,26,13,38,39,1,8,46,9,32,48,75,55,57,
+    56,58,59,49,60,19,34,61,66,14,47,50,65,54,52,51,15,69,53,18,68,67,70,74,71,72,98,77,76,78,79,16,17,118,82,73,84,85,
+    80,23,86,81,87,88,62,83,89,90,64,91,94,63,101,21,120,95,99,104,93,102,100,207,103,96,92,132,105,106,97,107,108,109,
+    111,112,110,123,121,122,113,114,117,125,126,115,124,116,127,128,129,130,137,134,136,131,140,141,133,172,142,135,
+    143,145,144,119,147,139,176,208,148,146,150,151,178,149,152,153,159,138,154,161,185,156,158,155,160,162,163,164,
+    157,186,167,171,165,306,263,168,174,169,182,285,184,282,177,181,173,179,188,253,180,170,183,199,175,201,187,274,
+    254,202,290,200,215,189,193,166,192,190,209,191,194,211,284,256,214,265,266,196,203,195,198,204,197,205,283,275,
+    210,212,213,216,219,255,217,276,220,218,222,224,221,225,206,223,229,227,231,226,230,240,239,241,232,237,233,243,
+    242,251,238,244,235,236,249,248,234,246,252,316,257,258,259,260,264,261,262,228,267,268,250,247,288,269,272,273,
+    279,270,245,277,271,278,286,294,314,281,289,287,336,292,295,293,280,296,298,3,445,299,300,297,302,301,304,305,315,
+    303,308,310,309,444,312,313,311,307,317,318,320,291,325,319,324,327,328,331,330,321,329,332,322,326,333,323,334,
+    339,337,370,335,377,368,369,375,385,340,386,359,342,344,345,341,358,346,348,343,376,349,351,353,352,350,355,361,
+    365,363,354,364,356,357,387,362,347,366,367,371,360,372,373,374,379,378,384,380,381,390,388,382,383,389,391,392,
+    393,394,395,396,433,401,400,398,399,404,408,402,406,409,410,405,412,403,407,413,415,414,411,417,416,451,418,420,
+    422,453,452,419,423,421,424,425,428,426,450,439,429,427,446,431,430,447,432,434,442,338,443,454,455,440,457,435,
+    448,456,441,436,449,458,459,437,438,461,462,463,397,465,460,464,466,468,467,469,471,470,474,475,472,473,478,481,
+    476,483,479,480,477,484,486,485,487,482]
 
 
 def V(name, c0, c1, step=1, p0=0, p1=128):
@@ -229,10 +249,6 @@ def rank_program(g, core, T, topo):
     def row(slot, bank):
         mm(bank, kq(K_R), ("TQ", 192 * slot + 8, 192 * slot + TW))
 
-    def rowtile(slot, hi, tot):
-        digits("tx", 8, TW, V("ki", 8, TW), C(hi), C(tot))
-        return lambda: quant("TQ", 192 * slot + 8, 192 * slot + TW, whole("tx", 8, TW))
-
     def opend(src, slot0, start):
         for b in range(4):
             mm(b, kq(slot0 + b), src, start, not start)
@@ -261,11 +277,15 @@ def rank_program(g, core, T, topo):
 
     def ubuild(l):
         for t in range(4):
-            act(sub("ub", t, 128 * l, 128 * l + 128), V("zf", 0, 128), FN.Identity, V("ut", 4 * l + t, 4 * l + t + 1))
+            src = V("ut", 4 * l + t, 4 * l + t + 1) if l < 2 else V("un", 4 * l - 8 + t, 4 * l - 7 + t)
+            act(sub("ub", t, 128 * l, 128 * l + 128), V("zf", 0, 128), FN.Identity, src)
 
-    KI = V("ki", 0, TW)
+    def uquant(l):
+        quant("UQ", 128 * l, 128 * l + 128, whole("ub", 128 * l, 128 * l + 128))
+
     K8 = V("ki", 0, 8)
     IDN = V("idn", 0, 128)
+    NUM = V("num", 0, 256)
     O_V, O_PA, O_L0, O_P1, O_L1, O_P2, O_S2, O_S1, O_S0, O_4 = 112, 96, 16, 24, 32, 40, 48, 56, 64, 128
     for h in range(2):
         dma("s", "dx%d" % h, [], [V("xt", 512 * h, 512 * h + 512)],
@@ -288,12 +308,9 @@ def rank_program(g, core, T, topo):
     sel(V("tp", 0, 128), V("zb", 0, 128), [[-1, 128]], OP.is_ge, TINY, 0, 1)
     iota(V("mk", 0, 128), [[0, 8], [-1, 4], [0, 4]], 4, 1)
     iota(V("mk", 128, 129), [[0, 1]], 0, 1)
+    iota(NUM, [[1, 256]], 0, 0)
     sel(V("kb", 0, 32), V("zf", 0, 32), [[4, 32]], OP.is_gt, 0.0625, 0, -1)
     sel(V("ki", TW, TY), V("kb", 0, 32), [[4, 32]], OP.is_ge, 0.0, 3, -1)
-    for h in range(2):
-        iota(K(4, 64 * h, 64 * h + 64), [[0, 1]], -1, -1)
-    for h in range(4):
-        iota(K(5, 32 * h, 32 * h + 32), [[0, 1]], -1, -1)
 
     memset(V("tmp", 128, 160), 0.0)
     memset(V("tmp", 288, 320), 0.0)
@@ -305,43 +322,38 @@ def rank_program(g, core, T, topo):
     ts(V("mj", 0, 128), V("mi", 0, 128), 15, OP.bitwise_and)
     kquant(K_A)
     ts(V("m16", 0, 128), V("mj", 0, 128), 0.0, OP.is_equal, 16.0, OP.mult)
-    kfill(K_SA, 0, -1.0, 0, 64)
-    kfill(K_SA, 0, 1.0, 64, 128)
-    memset(K(2, 0, 64), -63.0)
-    memset(K(2, 64, 128), 64.0)
-    for t in (1, 2, 3):
-        act(sub("kt", t, 128 * K_SA, 128 * K_SA + 128), V("zf", 0, 128), FN.Copy)
+    copy(K(2), V("mj", 0, 1))
     act(sub("kt", 3, 128 * K_R, 128 * K_R + 128), V("zf", 0, 128), FN.Copy)
     act(sub("kt", 2, 128 * K_R, 128 * K_R + 128), IDN, FN.Copy, None, 16.0)
     act(V("eqi", 128, 256), IDN, FN.Copy)
     for t, c in enumerate((-2.0 ** 30, 0.0, 2.0 ** 29, -2.0 ** 22)):
         afill(K_B, t, c)
-    for t, c in ((1, -256.0), (2, 0.0), (3, 0.0)):
-        afill(K_SB, t, c)
-    for h in range(4):
-        kfill(K_SB, 0, -1.0 if h % 2 == 0 else 1.0, 32 * h, 32 * h + 32)
-        memset(K(3, 32 * h, 32 * h + 32), -31.0 if h % 2 == 0 else 32.0)
     kfill(K_R, 0, 16.0)
     kfill(K_R, 1, 16.0)
     for t in range(4):
         act(sub("kt", t, 128 * K_16, 128 * K_16 + 128), V("m16", 0, 128), FN.Copy)
+    act(V("un", 0, 8), V("ut", 0, 8), FN.Copy, None, -1.0)
     ubuild(0)
 
     Q0, QA, QB = ("W0", 128, 384), ("W0", 128, 256), ("W0", 256, 384)
     d0, d1 = V("xs", 128, 129), V("xs", 288, 289)
     quant(*QA, whole("xt", 0, 128))
     mm(BC, QA, QA)
-    diag(BC, 0)
+    memset(whole("kt", 128 * K_SA, 128 * K_SA + 128), 0.0)
+    tt(V("tmp", 0, 128), PS(BC, 0, 128), IDN, OP.mult)
     quant(*QB, whole("xt", 128, 256))
+    scan(V("xs", 0, 160), V("tmp", 0, 160), V("tmp", 0, 160), 0.0, OP.max, OP.max)
     mm(BB, QB, QB)
     mm(BA, QA, QB)
     mm(0, QB, QA)
     act(V("g0", 0, 128), PS(BC, 0, 128), FN.Copy, None, 2.0 ** -40)
+    tt(V("tmp", 160, 288), PS(BB, 0, 128), IDN, OP.mult)
     turns(0, 0)
     for b in (1, 2, 3):
         act(V("rr", 0, 128, 1, 32 * b, 32 * b + 32), V("rr", 0, 128, 1, 0, 32), FN.Copy)
     act(V("df", 0, 128), V("rr", 0, 128), FN.Identity, d0, -1.0)
-    diag(BB, 160)
+    scan(V("xs", 160, 320), V("tmp", 160, 320), V("tmp", 160, 320), 0.0, OP.max, OP.max)
+    memset(whole("kt", 128 * K_SB, 128 * K_SB + 128), 0.0)
     turns(160, 128)
     for b in range(4):
         act(V("df", 128, 256, 1, 32 * b, 32 * b + 32), V("rr", 128, 256, 1, 0, 32), FN.Identity,
@@ -362,6 +374,7 @@ def rank_program(g, core, T, topo):
     ts(C(0), K(0), -1.0, OP.mult, -1.0, OP.add)
     kquant(K_E1)
     kquant(K_E1 + 1)
+    memset(V("npr", 0, 128), 1.0)
     ts(V("fl", 0, 256), PS(BD, 0, 256), 0.0, OP.is_lt)
     tt(V("gm", 0, 256), PS(BD, 0, 256), V("g0", 0, 256), OP.min)
     scan(V("sc", 0, 256), V("fl", 0, 256), V("zf", 0, 256), C(0), OP.add, OP.min)
@@ -372,6 +385,9 @@ def rank_program(g, core, T, topo):
     count("sc1", 256, V("sc1", 255, 256), C(3), C(4))
     count("sc2", 256, V("sc2", 255, 256), C(32), C(33))
     kquant(K_E1 + 2)
+    kfill(K_SA, 0, 1.0)
+    kfill(K_SB, 0, 1.0)
+    kfill(K_SB, 1, 256.0)
     ts(V("ml", 0, 129), V("mk", 0, 129), 3, OP.bitwise_and)
     for c0, hi, tot in ((16, 1, 2), (0, 3, 4), (8, 32, 33)):
         if c0 == 8:
@@ -382,6 +398,7 @@ def rank_program(g, core, T, topo):
             ts(sub("ts", 0, c0, c0 + 8), V("zf", 0, 8), C(hi), OP.add)
     kquant(K_EH)
     fin = carry("ts", 10, 128, BA, O_PA, 24)
+    ubuild(2)
     kquant(K_EH + 1)
     kquant(K_EH + 2)
     ts(V("m4", 0, 128), V("ml", 0, 128), 0.0, OP.is_equal, 64.0, OP.mult)
@@ -393,84 +410,84 @@ def rank_program(g, core, T, topo):
     pick(("PAR0", 0, 128), ("PARA", 0, 256), O_V, O_V + 8)
     opend(("V0", 0, 128), K_E1, True)
     opend(("PAR0", 0, 128), K_EH, False)
-    quant("UQ", 0, 128, whole("ub", 0, 128))
+    uquant(0)
+    uquant(2)
     kquant(K_SA)
-    memset(whole("tx", 0, TW), 0.0)
     anew(("E0", 0, 128), False)
     sent = send(0, ("E0", 0, 128), ("L0", 0, 128), rank ^ PART[0])
 
-    def choose(l, E, kw, thr, start, mask, hi, tot, slot, o0, gap):
-        u = ("UQ", 128 * l, 128 * l + 128)
-        mm(BC, u, E)
-        mm(BD, E, u)
+    def tally(c0, k, stay):
+        for c in range(k):
+            act(V("junk", 0, 128), V("sc", 128 * stay, 128 * stay + 128), FN.Sign, V("thr", c, c + 1),
+                1.0 if stay else -1.0, C(c0 + c))
+
+    def settle(o0, c0):
+        ts(V("off", o0, o0 + 4), V("col", c0, c0 + 4), 0.5, OP.mult, 64.0, OP.add)
+
+    def choose(l, E, kw, ties, k, c0, o0, gap):
+        mm(BC, ("UQ", 128 * l, 128 * l + 128), E, True, False)
+        mm(BC, E, ("UQ", 128 * l + 256, 128 * l + 384), False, True)
         gap(0)
-        if mask is None:
-            ts(V("df", 0, 128), PS(BC, 0, 128), PS(BD, 0, 1), OP.subtract)
-        else:
-            ts(V("df", 0, 128), PS(BC, 0, 128), PS(BD, 0, 1), OP.subtract, mask, OP.add)
+        tt(sub("ct", 0, 128, 256), PS(BC, 0, 128), V(ties, 0, 128), OP.is_lt)
         gap(3)
-        tt(sub("ct", 0, 128, 256), V("df", 0, 128), V("tp", 0, 128), OP.is_lt)
         quant("CQ", 128, 256, whole("ct", 128, 256))
         mm(BA, kq(kw), ("CQ", 128, 256))
         gap(1)
-        ts(V("fl", 0, 128), PS(BA, 0, 128), thr, OP.is_ge)
+        ts(V("fl", 0, 128), PS(BA, 0, 128), 16.0 * k - 0.5, OP.is_lt)
         gap(4)
-        scan(V("sc", 0, 128), V("fl", 0, 128), V("zf", 0, 128), start, OP.add, OP.min)
-        count("sc", 128, None, hi, tot)
+        scan(V("sc", 0, 128), V("fl", 0, 128), V("zf", 0, 128), 0.0, OP.add, OP.add)
+        scan(V("sc", 128, 256), V("fl", 0, 128), V("npr", 0, 128), 0.0, OP.add, OP.subtract)
+        tally(c0, k, 0)
+        tally(c0 + k, k, 1)
         gap(2)
-        digits("tx", 0, TW, KI, hi, tot)
-        carry("tx", slot, TW, BB, o0, 8)()
+        settle(o0, c0)
 
     pend = []
 
     def gap0(k):
         if k == 0:
-            pend.append(rowtile(1, 3, 4))
             kquant(K_R)
+            ubuild(3)
+            mm(0, ("E0", 0, 128), ("E0", 0, 128))
+            grab(V("pall", 0, 256), NUM, V("off", O_PA, O_PA + 16))
+            grab(V("lrv", 0, 128), NUM, V("off", O_V, O_V + 8))
+        if k == 3:
+            ts(V("thr", 0, 8), V("num", 0, 128, 16), K(2), OP.add, 0.5, OP.add)
         if k == 1:
-            pend.append(rowtile(9, 32, 33))
+            tt(V("tmp", 0, 128), PS(0, 0, 128), IDN, OP.mult)
             kquant(K_B)
             for t in range(4):
                 act(sub("k4", t, 0, 128), V("m4" if t < 2 else "zf", 0, 128), FN.Copy)
-        if k == 2:
-            mm(0, ("E0", 0, 128), ("E0", 0, 128))
-            tt(V("tmp", 0, 128), PS(0, 0, 128), IDN, OP.mult)
-            memset(whole("ty", 0, TY), 0.0)
+        if k == 4:
             scan(V("xs", 0, 160), V("tmp", 0, 160), V("tmp", 0, 160), 0.0, OP.max, OP.max)
-        if k > 2:
-            pend.pop()()
-    choose(0, ("E0", 0, 128), K_SA, K(2), K(4), None, C(5), C(6), 2, O_L0, gap0)
+        if k == 2:
+            turns(0, 0)
+            memset(whole("ty", 0, TY), 0.0)
+    choose(0, ("E0", 0, 128), K_SA, "tp", 4, 34, O_L0, gap0)
     sent += send_list(3, V("off", O_L0, O_L0 + 4), V("ofr", 0, 4), rank ^ PART[0])
     sel(V("bm", 0, 128, 1, 0, 64), V("zf", 0, 128, 1, 0, 64), [[1, 128]], OP.is_gt, 1.0, -63, 0)
     sel(V("bm", 0, 128, 1, 64, 128), V("zf", 0, 128, 1, 64, 128), [[-1, 128]], OP.is_gt, 1.0, 64, 0)
 
     mm(1, ("L0", 0, 128), ("L0", 0, 128))
-    turns(0, 0)
     tt(V("tmp", 160, 288), PS(1, 0, 128), IDN, OP.mult)
-    for b in (1, 2, 3):
-        act(V("rr", 0, 128, 1, 32 * b, 32 * b + 32), V("rr", 0, 128, 1, 0, 32), FN.Copy)
-    pick(("W1", 128, 192), ("E0", 0, 128), O_L0 + 4, O_L0 + 8)
+    copy(V("rr", 0, 128, 1, 32, 64), V("rr", 0, 128, 1, 0, 32))
     scan(V("xs", 160, 320), V("tmp", 160, 320), V("tmp", 160, 320), 0.0, OP.max, OP.max)
-    grab(V("r1", 0, 64), V("rr", 0, 128), V("off", O_L0 + 4, O_L0 + 8))
-    row(1, BC)
-    row(9, BD)
-    pend.append(rowtile(0, 1, 2))
+    settle(O_L0 + 4, 38)
+    for b in (2, 3):
+        act(V("rr", 0, 128, 1, 32 * b, 32 * b + 32), V("rr", 0, 128, 1, 0, 32), FN.Copy)
     turns(160, 128)
+    grab(V("r1", 0, 64), V("rr", 0, 128), V("off", O_L0 + 4, O_L0 + 8))
     copy(V("rr", 128, 256, 1, 32, 64), V("rr", 128, 256, 1, 0, 32))
     act(V("rr", 128, 256, 1, 64, 96), V("rr", 128, 256, 1, 0, 32), FN.Copy)
     copy(V("rr", 128, 256, 1, 96, 128), V("rr", 128, 256, 1, 0, 32))
+    pick(("W1", 128, 192), ("E0", 0, 128), O_L0 + 4, O_L0 + 8)
     upright(0)
     upright(1)
-    pend.pop()()
-    act(V("pall", 0, 128), PS(BC, 0, 128), FN.Copy)
-    act(V("pall", 128, 256), PS(BD, 0, 128), FN.Copy)
-    row(0, BD)
-    act(sub("ty", 2, 8, TW), IDN, FN.Copy, None, 16.0)
 
     def later(b, k):
         r = ("sc1", "sc2")[b]
         if k == 0:
-            ts(V("eqi", 0, 128), PS(BD, 0, 128), C(10 + b), OP.is_equal)
+            ts(V("eqi", 0, 128), V("lr0", 0, 128), C(10 + b), OP.is_equal)
         if k == 1:
             scan(V(r, 0, 256), V("eqi", 0, 256), V("eqi", 0, 256), 0.0, OP.max, OP.max)
         if k == 2:
@@ -506,6 +523,8 @@ def rank_program(g, core, T, topo):
         mm(BB, kq(kw), ("CQ", 0, 128))
         after(2)
         tt(V("gm", 0, 128), PS(BB, 0, 128), V("gd", 0, 128), OP.min)
+        if l == 1:
+            ts(V("npr", 0, 128), PS(BB, 0, 128), 0.0, OP.is_lt)
         scan(V("sc", 0, 128), V("gm", 0, 128), V("gm", 0, 128), LOW, OP.max, OP.max)
         count("sc", 128, V("sc", 127, 128), hi, tot)
         after(3)
@@ -525,13 +544,14 @@ def rank_program(g, core, T, topo):
 
     def after1(k):
         if k == 2:
-            quant("UQ", 128, 256, whole("ub", 128, 256))
-            kquant(K_4)
+            uquant(1)
             grab(V("prow", 0, 128), V("pall", 0, 256), V("off", O_V, O_V + 8))
+            act(sub("ty", 2, 8, TW), IDN, FN.Copy, None, 16.0)
+            kquant(K_4)
         if k == 3:
             kquant(K_SB)
             for b in range(2):
-                ts(V(("ebq", "fl")[b], 0, 128), PS(BD, 0, 128), K(b), OP.is_equal)
+                ts(V(("ebq", "fl")[b], 0, 128), V("lrv", 0, 128), K(b), OP.is_equal)
                 ts(V(("ea", "gm1")[b], 0, 128), V("prow", 0, 128), K(b), OP.is_equal)
         if k == 0:
             ts(C(14), C(13), K(0), OP.is_equal, BIG, OP.mult)
@@ -539,6 +559,7 @@ def rank_program(g, core, T, topo):
                 scan(V(("sc1", "sc2")[b], 0, 128), V(("ea", "gm1")[b], 0, 128), V(("ebq", "fl")[b], 0, 128), 0.0, OP.max, OP.max)
                 act(V("junk", 0, 128), V(("ebq", "fl")[b], 0, 128), FN.Copy, None, None, C(8 + b))
         if k == 4:
+            ts(V("tq", 0, 128), V("tp", 0, 128), C(14), OP.subtract)
             for b in range(2):
                 count(("sc1", "sc2")[b], 128, 1.0, None, C(10 + b))
             for t, c in enumerate((-2.0 ** 30, 0.0, 2.0 ** 29, -2.0 ** 23)):
@@ -547,6 +568,7 @@ def rank_program(g, core, T, topo):
             ts(sub("ct", 1, 128, 256), IDN, C(14), OP.mult, 1.0 / BIG, OP.mult)
             ts(C(15), C(13), K(0), OP.not_equal)
     F1 = ("W1", 128, 256)
+    uquant(3)
     grab(V("r1", 64, 128), V("rr", 128, 256), V("ofr", 0, 4))
     pick(("W1", 192, 256), ("L0", 0, 128), 0, 4, "ofr")
     front(F1, 1, K_B, C(12), C(13), 3, O_P1, O_4, ("E1", 0, 128), after1)
@@ -560,33 +582,34 @@ def rank_program(g, core, T, topo):
             pick(("PAR1", 0, 128), F1, O_P1, O_P1 + 8)
         if k == 3:
             ts(V("ea", 0, 128), PS(BB, 0, 128), K(0), OP.is_equal)
-        if k == 4:
+        if k == 1:
             scan(V("sc1", 0, 128), V("ea", 0, 128), V("ebq", 0, 128), 0.0, OP.max, OP.max)
             count("sc1", 128, 1.0, None, C(18))
-        if k == 1:
             kquant(K_C)
+        if k == 4:
             copy(V("k2", 0, 2), V("ki", 6, 8))
             copy(V("k2", 2, 4), V("ki", 0, 2))
         if k == 2:
             ts(sub("ts", 2, 0, 8), K8, C(15), OP.mult, 192.0, OP.mult)
-    choose(1, ("E1", 0, 128), K_SB, K(3), K(5), C(14), C(16), C(17), 4, O_L1, gap1)
+            memset(sub("ct", 0, 64, 128, 0, 64), 1.0)
+            memset(sub("ct", 0, 0, 64, 64, 128), 1.0)
+            quant("WQ", 0, 256, whole("wt", 0, 256))
+    choose(1, ("E1", 0, 128), K_SB, "tq", 2, 42, O_L1, gap1)
     pick(("SN1", 0, 64), ("E1", 0, 128), O_L1, O_L1 + 4)
     sent += send(1, ("SN1", 0, 64), ("W2", 160, 224), rank ^ PART[1])
+    grab(V("lr1", 0, 64), NUM, V("off", O_L1, O_L1 + 4))
+    settle(O_L1 + 4, 42)
     pick(("W2", 128, 160), ("E1", 0, 128), O_L1 + 2, O_L1 + 4)
     pick(("W2", 224, 256), ("E1", 0, 128), O_L1, O_L1 + 2)
 
-    row(4, BD)
+    ts(V("eqi", 64, 128), V("lr1", 0, 64), C(18), OP.is_equal)
     pick(("PR1", 0, 128), ("PAR1", 0, 128), O_L1, O_L1 + 8)
-    ts(V("eqi", 64, 128), PS(BD, 0, 64), C(18), OP.is_equal)
-    memset(sub("ct", 0, 64, 128, 0, 64), 1.0)
-    memset(sub("ct", 0, 0, 64, 64, 128), 1.0)
     scan(V("sc", 0, 192), V("eqi", 64, 256), V("eqi", 64, 256), 0.0, OP.max, OP.max)
     count("sc", 192, 1.0, C(19), C(20))
+    grab(V("lr0", 0, 128), NUM, V("off", O_L0, O_L0 + 8))
     add("v", [V("prow", 0, 128), V("off", O_V, O_V + 8)], [V("par", 0, 256)],
         lambda: g.vector.tensor_copy(T.par[:, 0:256].indirect(T.off[:, O_V:O_V + 8]), T.prow[:, 0:128]))
     dma("s", "dp0", [V("par", 0, 256)], [], lambda: T.pa[:, 0:256], lambda: T.par[0:1, 0:256])
-    row(2, BD)
-    quant("WQ", 0, 256, whole("wt", 0, 256))
 
     def after2(k):
         if k == 2:
@@ -620,7 +643,6 @@ def rank_program(g, core, T, topo):
     opend(("PR1", 0, 128), K_E1, True)
     pick(("W1", 256, 320), ("W2", 0, 384), O_S2, O_S2 + 4)
     opend(("W1", 192, 320), K_E1, False)
-    row(2, BD)
     anew(("W1", 0, 128), True)
     later(1, 0)
     pick(("SND", 0, 64), ("W1", 64, 320), O_S1 + 4, O_S1 + 8)
@@ -653,6 +675,8 @@ def rank_program(g, core, T, topo):
         copy(V("ysb", 256 + 128 * h, 384 + 128 * h), PS(BB + 2 * h, 0, 128))
     dma("a", "dy0", [V("ysb", 0, 512)], [], lambda: T.y[:, :], lambda: T.ysb[:, :])
 
+    assert sorted(ISSUE) == list(range(len(ops)))
+    ops = [ops[n] for n in ISSUE]
     know = {q: {} for q in queue}
     for n, o in enumerate(ops):
         o["clock"] = o["q"] if o["kind"] == "c" else n

from concourse.mybir import dt, AluOpType, ActivationFunctionType

OP = AluOpType
FN = ActivationFunctionType
PART = [1, 4]
TW = 136
TY = 168
BIG = 2.0 ** 90
TINY = 2.0 ** -100
LOW = -1.0e29

PAIRS = {"W0": 512, "W1": 320, "W2": 384, "V0": 128, "PAR0": 128, "PR0": 128, "PAR1": 128, "PR1": 128, "PAR2": 128,
         "E0": 128, "E1": 128, "L0": 128, "SN1": 64, "SND": 64, "FIN": 256, "UQ": 512, "WQ": 256, "PARA": 256,
         "KQ": 2048, "CQ": 256, "TQ": 2112}
SCRATCH = {}
for _n, _w in PAIRS.items():
    SCRATCH["q" + _n] = ("sbuf", [128, _w], "float8_e4m3fn_x4")
    SCRATCH["s" + _n] = ("sbuf", [128, _w], "uint8")
for _n, _w in {"xt": 1024, "wt": 1024, "ut": 16, "ub": 2048, "zb": 520, "eb": 2080, "kt": 3584, "k4": 512, "ct": 1024,
               "ty": 4 * TY, "ts": 512, "ht": 512, "tn": 128, "tp": 128, "tq": 128, "df": 256, "junk": 6144}.items():
    SCRATCH[_n] = ("sbuf", [128, _w], "bfloat16")
for _n, _w in {"zf": 256, "idn": 128, "ki": TY, "kb": 32, "g0": 256, "g1": 256, "gm1": 256, "sc1": 256, "sc2": 256,
               "pall": 256, "dv": 512, "dh": 512, "m4": 128, "r1": 128, "xc": 32, "bm": 128, "k2": 8, "ka": 8,
               "tmp": 320, "xs": 320, "rr": 256, "gs": 128, "gd": 128, "gm": 256, "sc": 256, "fl": 256, "eqi": 256,
               "ea": 128, "ebq": 128, "col": 48, "cst": 8, "par": 256, "prow": 128, "ysb": 512, "m16": 128,
               "num": 256, "thr": 8, "un": 8, "npr": 128, "lrv": 128, "lr0": 128, "lr1": 64}.items():
    SCRATCH[_n] = ("sbuf", [128, _w], "float32")
for _n in ("mi", "mj", "mk", "ml"):
    SCRATCH[_n] = ("sbuf", [128, 136], "int32")
SCRATCH["off"] = ("sbuf", [128, 192], "uint16")
SCRATCH["ofr"] = ("sbuf", [128, 8], "uint16")
SCRATCH["ps"] = ("psum", [128, 4096], "float32")
DMAS = ["dx0", "dx1", "du", "dw", "dp0", "dp1", "dp2", "doc", "ds0", "ds1", "ds2", "ds3", "dy0"]
SEMAPHORES = ["cv", "ca", "cp", "cg", "arr0", "arr1", "arr2", "arr3", "snt"] + DMAS

K_A, K_16, K_SA, K_R, K_B, K_SB, K_C, K_E1, K_EH, K_4 = 0, 1, 2, 3, 4, 5, 6, 7, 11, 15
BA, BB, BC, BD = 4, 5, 6, 7

ISSUE = [
    0,20,4,7,24,2,29,6,31,25,42,40,12,45,44,30,41,28,27,11,33,10,37,22,5,35,43,36,26,13,38,39,1,8,46,9,32,48,75,55,57,
    56,58,59,49,60,19,34,61,66,14,47,50,65,54,52,51,15,69,53,18,68,67,70,74,71,72,98,77,76,78,79,16,17,118,82,73,84,85,
    80,23,86,81,87,88,62,83,89,90,64,91,94,63,101,21,120,95,99,104,93,102,100,207,103,96,92,132,105,106,97,107,108,109,
    111,112,110,123,121,122,113,114,117,125,126,115,124,116,127,128,129,130,137,134,136,131,140,141,133,172,142,135,
    143,145,144,119,147,139,176,208,148,146,150,151,178,149,152,153,159,138,154,161,185,156,158,155,160,162,163,164,
    157,186,167,171,165,306,263,168,174,169,182,285,184,282,177,181,173,179,188,253,180,170,183,199,175,201,187,274,
    254,202,290,200,215,189,193,166,192,190,209,191,194,211,284,256,214,265,266,196,203,195,198,204,197,205,283,275,
    210,212,213,216,219,255,217,276,220,218,222,224,221,225,206,223,229,227,231,226,230,240,239,241,232,237,233,243,
    242,251,238,244,235,236,249,248,234,246,252,316,257,258,259,260,264,261,262,228,267,268,250,247,288,269,272,273,
    279,270,245,277,271,278,286,294,314,281,289,287,336,292,295,293,280,296,298,3,445,299,300,297,302,301,304,305,315,
    303,308,310,309,444,312,313,311,307,317,318,320,291,325,319,324,327,328,331,330,321,329,332,322,326,333,323,334,
    339,337,370,335,377,368,369,375,385,340,386,359,342,344,345,341,358,346,348,343,376,349,351,353,352,350,355,361,
    365,363,354,364,356,357,387,362,347,366,367,371,360,372,373,374,379,378,384,380,381,390,388,382,383,389,391,392,
    393,394,395,396,433,401,400,398,399,404,408,402,406,409,410,405,412,403,407,413,415,414,411,417,416,451,418,420,
    422,453,452,419,423,421,424,425,428,426,450,439,429,427,446,431,430,447,432,434,442,338,443,454,455,440,457,435,
    448,456,441,436,449,458,459,437,438,461,462,463,397,465,460,464,466,468,467,469,471,470,474,475,472,473,478,481,
    476,483,479,480,477,484,486,485,487,482]


def V(name, c0, c1, step=1, p0=0, p1=128):
    return (name, p0, p1, c0, c1, step)


def PS(bank, c0, c1, step=1):
    return V("ps", 512 * bank + c0, 512 * bank + c1, step)


def clash(a, b):
    if a[0] != b[0]:
        return False
    if a[0] == "ps":
        return a[3] // 512 == b[3] // 512
    if a[2] <= b[1] or b[2] <= a[1] or a[4] <= b[3] or b[4] <= a[3]:
        return False
    if a[5] == b[5] and a[5] > 1:
        return (a[3] - b[3]) % a[5] == 0
    return True


def rank_program(g, core, T, topo):
    rank = T.rank_of(core)
    if rank is None:
        return
    ops = []
    spare = [0]
    queue = {"v": g.vector, "a": g.scalar, "p": g.tensor, "g": g, "s": g.sync}

    def ap(v):
        if not isinstance(v, tuple):
            return v
        if v[5] == 1:
            return T[v[0]][v[1]:v[2], v[3]:v[4]]
        return T[v[0]][v[1]:v[2], v[3]:v[4]:v[5]]

    def views(*xs):
        return [x for x in xs if isinstance(x, tuple)]

    def add(q, reads, writes, fn, sem=None, kind="c"):
        ops.append({"q": q, "r": reads, "w": writes, "fn": fn, "sem": sem, "kind": kind})

    def memset(o, c):
        add("v", [], [o], lambda: g.vector.memset(ap(o), c))

    def copy(o, i):
        add("v", [i], [o], lambda: g.vector.tensor_copy(ap(o), ap(i)))

    def tt(o, a, b, op):
        add("v", [a, b], [o], lambda: g.vector.tensor_tensor(ap(o), ap(a), ap(b), op))

    def ts(o, a, s1, op0, s2=None, op1=None):
        if op1 is None:
            add("v", views(a, s1), [o], lambda: g.vector.tensor_scalar(ap(o), ap(a), ap(s1), None, op0))
        else:
            add("v", views(a, s1, s2), [o], lambda: g.vector.tensor_scalar(ap(o), ap(a), ap(s1), ap(s2), op0, op1))

    def scan(o, a, b, init, op0, op1):
        add("v", views(a, b, init), [o], lambda: g.vector.tensor_tensor_scan(ap(o), ap(a), ap(b), ap(init), op0, op1))

    def turn(o, i):
        add("v", [i], [o], lambda: g.vector.transpose(ap(o), ap(i)))

    def act(o, i, fn, bias=None, scale=None, acc=None):
        kw = {}
        if bias is not None:
            kw["bias"] = bias
        if scale is not None:
            kw["scale"] = scale
        if acc is not None:
            kw["accum_out"] = acc
        if o[0] == "junk":
            o = V("junk", spare[0], spare[0] + o[4])
            spare[0] = o[4]
        add("a", views(i, bias, scale), views(o, acc),
            lambda: g.scalar.activation(ap(o), ap(i), fn, **{k: ap(x) for k, x in kw.items()}))

    def grab(o, win, of):
        add("a", [win, of], [o], lambda: g.scalar.activation(ap(o), ap(win).indirect(ap(of)), FN.Copy))

    def pool(reads, o, fn):
        turn_ = V("pool", 0, 1)
        if o[2] - o[1] < 128:
            add("g", reads, [o, turn_], fn)
        else:
            add("g", reads + [turn_], [o], fn)

    def iota(o, pat, base, cm):
        if o[0] in ("mi", "mk"):
            pool([], o, lambda: g.iota(ap(o), pat, base, cm))
        else:
            pool([], o, lambda: g.iota(ap(o), pat, base, cm, allow_small_or_imprecise_dtypes=True))

    def sel(o, i, pat, op, fill, base, cm):
        pool([i], o, lambda: g.affine_select(ap(o), ap(i), pat, op, fill, base, cm))

    def pq(n, a, b):
        return V("q" + n, a, b), V("s" + n, a, b)

    def quant(n, a, b, tile):
        q, s = pq(n, a, b)
        add("v", [tile], [q, s], lambda: g.vector.quantize_mx(ap(q), ap(s), ap(tile)))

    def mm(bank, w, x, start=True, stop=True):
        qw, sw = pq(*w)
        qx, sx = pq(*x)
        o = PS(bank, 0, x[2] - x[1])
        add("p", [qw, sw, qx, sx], [o],
            lambda: g.tensor.matmul_mx(ap(o), ap(qw), ap(sw), ap(qx), ap(sx), start, stop))

    def kq(slot):
        return ("KQ", 128 * slot, 128 * slot + 128)

    def pick(dst, win, o0, o1, lists="off"):
        qd, sd = pq(*dst)
        qw, sw = pq(*win)
        of = V(lists, o0, o1)
        add("v", [qw, of], [qd], lambda: g.vector.tensor_copy(
            ap(qd).bitcast(dt.uint32), ap(qw).bitcast(dt.uint32).indirect(ap(of))))
        grab(sd, sw, of)

    def dma(q, sem, reads, writes, out, in_):
        add(q, reads, writes, lambda: queue[q].dma_start(out(), in_()), sem, "d")

    def send(k, src, dst, peer_rank):
        peer = T.cores[peer_rank]
        rid, pid, _ = topo.addr(peer)
        mask = topo.mask(core, peer)
        qs, ss = pq(*src)
        qd, sd = pq(*dst)
        sem = T.sem["arr%d" % k]
        add("g", [qs], [], lambda: g.remote_dma(ap(qd).bitcast(dt.uint8), ap(qs).bitcast(dt.uint8), sem, T.sem.snt,
                                                pid, rid, mask), None, "r")
        add("g", [ss], [], lambda: g.remote_dma(ap(sd), ap(ss), sem, T.sem.snt, pid, rid, mask), None, "r")
        n = 2 * len(topo.engines(peer, core))
        add(None, [], [qd, sd], None, ("arr%d" % k, n), "x")
        return 2 * len(topo.engines(core, peer))

    def send_list(k, src, dst, peer_rank):
        peer = T.cores[peer_rank]
        rid, pid, _ = topo.addr(peer)
        add("g", [src], [], lambda: g.remote_dma(ap(dst), ap(src), T.sem["arr%d" % k], T.sem.snt, pid, rid,
                                                 topo.mask(core, peer)), None, "r")
        add(None, [], [dst], None, ("arr%d" % k, len(topo.engines(peer, core))), "x")
        return len(topo.engines(core, peer))

    def C(k):
        return V("col", k, k + 1)

    def K(k, p0=0, p1=128):
        return V("cst", k, k + 1, 1, p0, p1)

    def sub(tile, t, c0, c1, p0=0, p1=128):
        return V(tile, 4 * c0 + t, 4 * c1, 4, p0, p1)

    def whole(tile, c0, c1):
        return V(tile, 4 * c0, 4 * c1)

    def kfill(slot, t, c, c0=0, c1=128, p0=0, p1=128):
        memset(sub("kt", t, 128 * slot + c0, 128 * slot + c1, p0, p1), c)

    def afill(slot, t, c):
        act(sub("kt", t, 128 * slot, 128 * slot + 128), V("zf", 0, 128), FN.Identity, c)

    def kquant(slot):
        if slot < K_E1:
            quant("KQ", 128 * slot, 128 * slot + 128, whole("kt", 128 * slot, 128 * slot + 128))
        elif slot == K_4:
            quant("KQ", 128 * slot, 128 * slot + 128, whole("k4", 0, 128))
        else:
            h, b = divmod(slot - K_E1, 4)
            at = 520 * (2 * h + b % 2) + (2 - b // 2 * 2)
            quant("KQ", 128 * slot, 128 * slot + 128, V("eb", at, at + 512))

    def count(r, n, bias, hi, tot):
        if hi is not None:
            act(V("junk", 0, n // 16), V(r, 15, n, 16), FN.Sign, bias, -1.0, hi)
        act(V("junk", 0, n), V(r, 0, n), FN.Sign, bias, -1.0, tot)

    def digits(tile, c0, c1, kc, hi, tot):
        ts(sub(tile, 1, c0, c1), kc, tot, OP.mult, hi, OP.subtract)
        act(sub(tile, 0, c0, c1), V("zf", 0, c1 - c0), FN.Identity, hi)

    def carry(tile, slot, n, bank, o0, k):
        quant("TQ", 192 * slot, 192 * slot + n, whole(tile, 0, n))
        mm(bank, kq(K_16), ("TQ", 192 * slot, 192 * slot + 128))

        def fin():
            copy(V("off", o0, o0 + k), PS(bank, 0, k))
        return fin

    def row(slot, bank):
        mm(bank, kq(K_R), ("TQ", 192 * slot + 8, 192 * slot + TW))

    def opend(src, slot0, start):
        for b in range(4):
            mm(b, kq(slot0 + b), src, start, not start)

    def anew(dst, half):
        for b in range(4):
            o, i = sub("ht", b, 0, 128), PS(b, 0, 128)
            if b % 2 == 0:
                act(o, i, FN.Copy, None, 0.5 if half else None)
            elif half:
                ts(o, i, 0.5, OP.mult)
            else:
                copy(o, i)
        quant(*dst, whole("ht", 0, 128))

    def diag(bank, at):
        tt(V("tmp", at, at + 128), PS(bank, 0, 128), V("idn", 0, 128), OP.mult)
        scan(V("xs", at, at + 160), V("tmp", at, at + 160), V("tmp", at, at + 160), 0.0, OP.max, OP.max)

    def turns(at, to):
        for a in range(4):
            turn(V("rr", to + 32 * a, to + 32 * a + 32, 1, 0, 32), V("xs", at + 128, at + 160, 1, 32 * a, 32 * a + 32))

    def upright(a):
        turn(V("xc", 0, 32, 1, 32 * a, 32 * a + 32), V("r1", 32 * a, 32 * a + 32, 1, 0, 32))

    def ubuild(l):
        for t in range(4):
            src = V("ut", 4 * l + t, 4 * l + t + 1) if l < 2 else V("un", 4 * l - 8 + t, 4 * l - 7 + t)
            act(sub("ub", t, 128 * l, 128 * l + 128), V("zf", 0, 128), FN.Identity, src)

    def uquant(l):
        quant("UQ", 128 * l, 128 * l + 128, whole("ub", 128 * l, 128 * l + 128))

    K8 = V("ki", 0, 8)
    IDN = V("idn", 0, 128)
    NUM = V("num", 0, 256)
    O_V, O_PA, O_L0, O_P1, O_L1, O_P2, O_S2, O_S1, O_S0, O_4 = 112, 96, 16, 24, 32, 40, 48, 56, 64, 128
    for h in range(2):
        dma("s", "dx%d" % h, [], [V("xt", 512 * h, 512 * h + 512)],
            lambda h=h: T.xt[:, 512 * h:512 * h + 512], lambda h=h: T.x[:, 512 * h:512 * h + 512])
    dma("a", "du", [], [V("ut", 0, 8)], lambda: T.ut[:, 0:8], lambda: T.u[:, 0:8])
    dma("s", "dw", [V("xt", 512, 1024)], [V("wt", 0, 1024)], lambda: T.wt[:, :], lambda: T.w[:, :])

    memset(V("zf", 0, 256), 0.0)
    memset(V("zb", 0, 520), 0.0)
    sel(IDN, V("zf", 0, 128), [[-1, 128]], OP.not_equal, 1.0, 0, 1)
    iota(V("mi", 0, 128), [[-1, 128]], 128, 1)
    sel(V("tn", 0, 128), V("zb", 0, 128), [[-1, 128]], OP.is_ge, -TINY, 0, 1)
    sel(V("ki", 8, TW), V("zf", 0, 128), [[-1, 128]], OP.not_equal, 0.0625, 0, 1)
    sel(V("ka", 0, 8), V("zf", 0, 8), [[16, 8]], OP.is_gt, 0.0625, 0, -1)
    iota(K(0), [[0, 1]], 0, 1)
    iota(K(1), [[0, 1]], 128, 1)
    sel(K8, V("ka", 0, 8), [[16, 8]], OP.is_ge, 0.0, 15, -1)
    for j, (at, c) in enumerate(((2, 1.0), (3, 1.0), (2, -0.5), (3, -0.5))):
        sel(V("eb", 520 * j, 520 * j + 520), V("zb", 0, 520), [[-1, 520]], OP.not_equal, c, at, 4)
    sel(V("tp", 0, 128), V("zb", 0, 128), [[-1, 128]], OP.is_ge, TINY, 0, 1)
    iota(V("mk", 0, 128), [[0, 8], [-1, 4], [0, 4]], 4, 1)
    iota(V("mk", 128, 129), [[0, 1]], 0, 1)
    iota(NUM, [[1, 256]], 0, 0)
    sel(V("kb", 0, 32), V("zf", 0, 32), [[4, 32]], OP.is_gt, 0.0625, 0, -1)
    sel(V("ki", TW, TY), V("kb", 0, 32), [[4, 32]], OP.is_ge, 0.0, 3, -1)

    memset(V("tmp", 128, 160), 0.0)
    memset(V("tmp", 288, 320), 0.0)
    memset(sub("ct", 2, 0, 256), 1.0)
    memset(sub("ct", 3, 0, 256), 1.0)
    for t, c in enumerate((-2.0 ** 30, -2.0 ** 30, 2.0 ** 30, -2.0 ** 22)):
        kfill(K_A, t, c)
    memset(whole("ts", 0, 128), 0.0)
    ts(V("mj", 0, 128), V("mi", 0, 128), 15, OP.bitwise_and)
    kquant(K_A)
    ts(V("m16", 0, 128), V("mj", 0, 128), 0.0, OP.is_equal, 16.0, OP.mult)
    copy(K(2), V("mj", 0, 1))
    act(sub("kt", 3, 128 * K_R, 128 * K_R + 128), V("zf", 0, 128), FN.Copy)
    act(sub("kt", 2, 128 * K_R, 128 * K_R + 128), IDN, FN.Copy, None, 16.0)
    act(V("eqi", 128, 256), IDN, FN.Copy)
    for t, c in enumerate((-2.0 ** 30, 0.0, 2.0 ** 29, -2.0 ** 22)):
        afill(K_B, t, c)
    kfill(K_R, 0, 16.0)
    kfill(K_R, 1, 16.0)
    for t in range(4):
        act(sub("kt", t, 128 * K_16, 128 * K_16 + 128), V("m16", 0, 128), FN.Copy)
    act(V("un", 0, 8), V("ut", 0, 8), FN.Copy, None, -1.0)
    ubuild(0)

    Q0, QA, QB = ("W0", 128, 384), ("W0", 128, 256), ("W0", 256, 384)
    d0, d1 = V("xs", 128, 129), V("xs", 288, 289)
    quant(*QA, whole("xt", 0, 128))
    mm(BC, QA, QA)
    memset(whole("kt", 128 * K_SA, 128 * K_SA + 128), 0.0)
    tt(V("tmp", 0, 128), PS(BC, 0, 128), IDN, OP.mult)
    quant(*QB, whole("xt", 128, 256))
    scan(V("xs", 0, 160), V("tmp", 0, 160), V("tmp", 0, 160), 0.0, OP.max, OP.max)
    mm(BB, QB, QB)
    mm(BA, QA, QB)
    mm(0, QB, QA)
    act(V("g0", 0, 128), PS(BC, 0, 128), FN.Copy, None, 2.0 ** -40)
    tt(V("tmp", 160, 288), PS(BB, 0, 128), IDN, OP.mult)
    turns(0, 0)
    for b in (1, 2, 3):
        act(V("rr", 0, 128, 1, 32 * b, 32 * b + 32), V("rr", 0, 128, 1, 0, 32), FN.Copy)
    act(V("df", 0, 128), V("rr", 0, 128), FN.Identity, d0, -1.0)
    scan(V("xs", 160, 320), V("tmp", 160, 320), V("tmp", 160, 320), 0.0, OP.max, OP.max)
    memset(whole("kt", 128 * K_SB, 128 * K_SB + 128), 0.0)
    turns(160, 128)
    for b in range(4):
        act(V("df", 128, 256, 1, 32 * b, 32 * b + 32), V("rr", 128, 256, 1, 0, 32), FN.Identity,
            V("xs", 288, 289, 1, 32 * b, 32 * b + 32), -1.0)
    ts(sub("ct", 1, 0, 128), V("rr", 0, 128), d1, OP.is_lt)
    for b in (1, 2, 3):
        copy(V("rr", 128, 256, 1, 32 * b, 32 * b + 32), V("rr", 128, 256, 1, 0, 32))
    tt(sub("ct", 0, 0, 128), V("df", 0, 128), V("tn", 0, 128), OP.is_gt)
    ts(sub("ct", 0, 128, 256), V("rr", 128, 256), d0, OP.is_le)
    tt(sub("ct", 1, 128, 256), V("df", 128, 256), V("tn", 0, 128), OP.is_gt)
    act(V("g0", 128, 256), PS(BA, 0, 128), FN.Copy, None, 2.0 ** -40)
    act(V("g1", 0, 128), PS(0, 0, 128), FN.Copy, None, 2.0 ** -40)
    act(V("g1", 128, 256), PS(BB, 0, 128), FN.Copy, None, 2.0 ** -40)
    ubuild(1)
    kquant(K_16)
    quant("CQ", 0, 256, whole("ct", 0, 256))
    mm(BD, kq(K_A), ("CQ", 0, 256))
    ts(C(0), K(0), -1.0, OP.mult, -1.0, OP.add)
    kquant(K_E1)
    kquant(K_E1 + 1)
    memset(V("npr", 0, 128), 1.0)
    ts(V("fl", 0, 256), PS(BD, 0, 256), 0.0, OP.is_lt)
    tt(V("gm", 0, 256), PS(BD, 0, 256), V("g0", 0, 256), OP.min)
    scan(V("sc", 0, 256), V("fl", 0, 256), V("zf", 0, 256), C(0), OP.add, OP.min)
    tt(V("gm1", 0, 256), PS(BD, 0, 256), V("g1", 0, 256), OP.min)
    scan(V("sc1", 0, 256), V("gm", 0, 256), V("gm", 0, 256), LOW, OP.max, OP.max)
    scan(V("sc2", 0, 256), V("gm1", 0, 256), V("gm1", 0, 256), LOW, OP.max, OP.max)
    count("sc", 256, None, C(1), C(2))
    count("sc1", 256, V("sc1", 255, 256), C(3), C(4))
    count("sc2", 256, V("sc2", 255, 256), C(32), C(33))
    kquant(K_E1 + 2)
    kfill(K_SA, 0, 1.0)
    kfill(K_SB, 0, 1.0)
    kfill(K_SB, 1, 256.0)
    ts(V("ml", 0, 129), V("mk", 0, 129), 3, OP.bitwise_and)
    for c0, hi, tot in ((16, 1, 2), (0, 3, 4), (8, 32, 33)):
        if c0 == 8:
            kquant(K_E1 + 3)
            digits("ts", c0, c0 + 8, K8, C(hi), C(tot))
        else:
            ts(sub("ts", 1, c0, c0 + 8), K8, C(tot), OP.mult, C(hi), OP.subtract)
            ts(sub("ts", 0, c0, c0 + 8), V("zf", 0, 8), C(hi), OP.add)
    kquant(K_EH)
    fin = carry("ts", 10, 128, BA, O_PA, 24)
    ubuild(2)
    kquant(K_EH + 1)
    kquant(K_EH + 2)
    ts(V("m4", 0, 128), V("ml", 0, 128), 0.0, OP.is_equal, 64.0, OP.mult)
    copy(K(6), V("ml", 128, 129))
    fin()
    kquant(K_EH + 3)
    pick(("PARA", 0, 256), Q0, O_PA, O_PA + 16)
    pick(("V0", 0, 128), Q0, O_V, O_V + 8)
    pick(("PAR0", 0, 128), ("PARA", 0, 256), O_V, O_V + 8)
    opend(("V0", 0, 128), K_E1, True)
    opend(("PAR0", 0, 128), K_EH, False)
    uquant(0)
    uquant(2)
    kquant(K_SA)
    anew(("E0", 0, 128), False)
    sent = send(0, ("E0", 0, 128), ("L0", 0, 128), rank ^ PART[0])

    def tally(c0, k, stay):
        for c in range(k):
            act(V("junk", 0, 128), V("sc", 128 * stay, 128 * stay + 128), FN.Sign, V("thr", c, c + 1),
                1.0 if stay else -1.0, C(c0 + c))

    def settle(o0, c0):
        ts(V("off", o0, o0 + 4), V("col", c0, c0 + 4), 0.5, OP.mult, 64.0, OP.add)

    def choose(l, E, kw, ties, k, c0, o0, gap):
        mm(BC, ("UQ", 128 * l, 128 * l + 128), E, True, False)
        mm(BC, E, ("UQ", 128 * l + 256, 128 * l + 384), False, True)
        gap(0)
        tt(sub("ct", 0, 128, 256), PS(BC, 0, 128), V(ties, 0, 128), OP.is_lt)
        gap(3)
        quant("CQ", 128, 256, whole("ct", 128, 256))
        mm(BA, kq(kw), ("CQ", 128, 256))
        gap(1)
        ts(V("fl", 0, 128), PS(BA, 0, 128), 16.0 * k - 0.5, OP.is_lt)
        gap(4)
        scan(V("sc", 0, 128), V("fl", 0, 128), V("zf", 0, 128), 0.0, OP.add, OP.add)
        scan(V("sc", 128, 256), V("fl", 0, 128), V("npr", 0, 128), 0.0, OP.add, OP.subtract)
        tally(c0, k, 0)
        tally(c0 + k, k, 1)
        gap(2)
        settle(o0, c0)

    pend = []

    def gap0(k):
        if k == 0:
            kquant(K_R)
            ubuild(3)
            mm(0, ("E0", 0, 128), ("E0", 0, 128))
            grab(V("pall", 0, 256), NUM, V("off", O_PA, O_PA + 16))
            grab(V("lrv", 0, 128), NUM, V("off", O_V, O_V + 8))
        if k == 3:
            ts(V("thr", 0, 8), V("num", 0, 128, 16), K(2), OP.add, 0.5, OP.add)
        if k == 1:
            tt(V("tmp", 0, 128), PS(0, 0, 128), IDN, OP.mult)
            kquant(K_B)
            for t in range(4):
                act(sub("k4", t, 0, 128), V("m4" if t < 2 else "zf", 0, 128), FN.Copy)
        if k == 4:
            scan(V("xs", 0, 160), V("tmp", 0, 160), V("tmp", 0, 160), 0.0, OP.max, OP.max)
        if k == 2:
            turns(0, 0)
            memset(whole("ty", 0, TY), 0.0)
    choose(0, ("E0", 0, 128), K_SA, "tp", 4, 34, O_L0, gap0)
    sent += send_list(3, V("off", O_L0, O_L0 + 4), V("ofr", 0, 4), rank ^ PART[0])
    sel(V("bm", 0, 128, 1, 0, 64), V("zf", 0, 128, 1, 0, 64), [[1, 128]], OP.is_gt, 1.0, -63, 0)
    sel(V("bm", 0, 128, 1, 64, 128), V("zf", 0, 128, 1, 64, 128), [[-1, 128]], OP.is_gt, 1.0, 64, 0)

    mm(1, ("L0", 0, 128), ("L0", 0, 128))
    tt(V("tmp", 160, 288), PS(1, 0, 128), IDN, OP.mult)
    copy(V("rr", 0, 128, 1, 32, 64), V("rr", 0, 128, 1, 0, 32))
    scan(V("xs", 160, 320), V("tmp", 160, 320), V("tmp", 160, 320), 0.0, OP.max, OP.max)
    settle(O_L0 + 4, 38)
    for b in (2, 3):
        act(V("rr", 0, 128, 1, 32 * b, 32 * b + 32), V("rr", 0, 128, 1, 0, 32), FN.Copy)
    turns(160, 128)
    grab(V("r1", 0, 64), V("rr", 0, 128), V("off", O_L0 + 4, O_L0 + 8))
    copy(V("rr", 128, 256, 1, 32, 64), V("rr", 128, 256, 1, 0, 32))
    act(V("rr", 128, 256, 1, 64, 96), V("rr", 128, 256, 1, 0, 32), FN.Copy)
    copy(V("rr", 128, 256, 1, 96, 128), V("rr", 128, 256, 1, 0, 32))
    pick(("W1", 128, 192), ("E0", 0, 128), O_L0 + 4, O_L0 + 8)
    upright(0)
    upright(1)

    def later(b, k):
        r = ("sc1", "sc2")[b]
        if k == 0:
            ts(V("eqi", 0, 128), V("lr0", 0, 128), C(10 + b), OP.is_equal)
        if k == 1:
            scan(V(r, 0, 256), V("eqi", 0, 256), V("eqi", 0, 256), 0.0, OP.max, OP.max)
        if k == 2:
            count(r, 256, 1.0, C(26 + 2 * b), C(27 + 2 * b))

    def front(F, l, kw, hi, tot, slot, o0, o4c, E, after):
        mm(BA, F, F)
        for b in range(4):
            mm(b, kq(K_E1 + b), F)
        if l == 2:
            diag(BA, 0)
        act(V("gs", 0, 128), PS(BA, 0, 128), FN.Copy, None, 2.0 ** -40)
        sel(V("gd", 0, 128), V("gs", 0, 128), [[-1, 128]], OP.not_equal, 3.0 * 2.0 ** 27, 0, 1)
        if l == 1:
            upright(2)
            upright(3)
            ts(V("df", 0, 128), V("r1", 0, 128), V("xc", 0, 1), OP.subtract, -1.0, OP.mult)
            tt(sub("ct", 0, 0, 128), V("df", 0, 128), V("tn", 0, 128), OP.is_gt)
        else:
            turn(V("xc", 0, 32), V("xs", 128, 160))
            ts(V("df", 0, 32), V("xc", 0, 32), V("xs", 128, 129), OP.subtract, -1.0, OP.mult)
            for a in range(4):
                b = a ^ 1
                ts(sub("ct", 0, 32 * b, 32 * b + 32, 32 * a, 32 * a + 32), V("xc", 0, 32, 1, 32 * b, 32 * b + 32),
                   V("xs", 128, 129, 1, 32 * a, 32 * a + 32), OP.is_le if a < b else OP.is_lt)
            for a in range(4):
                tt(sub("ct", 0, 32 * a, 32 * a + 32, 32 * a, 32 * a + 32), V("df", 0, 32, 1, 32 * a, 32 * a + 32),
                   V("tn", 32 * a, 32 * a + 32, 1, 32 * a, 32 * a + 32), OP.is_gt)
        for b in range(4):
            act(sub("dv", b, 0, 128), PS(b, 0, 128), FN.Copy)
            act(sub("dh", b, 0, 128), PS(b, 0, 128), FN.Copy, None, -0.5)
        quant("CQ", 0, 128, whole("ct", 0, 128))
        mm(BB, kq(kw), ("CQ", 0, 128))
        after(2)
        tt(V("gm", 0, 128), PS(BB, 0, 128), V("gd", 0, 128), OP.min)
        if l == 1:
            ts(V("npr", 0, 128), PS(BB, 0, 128), 0.0, OP.is_lt)
        scan(V("sc", 0, 128), V("gm", 0, 128), V("gm", 0, 128), LOW, OP.max, OP.max)
        count("sc", 128, V("sc", 127, 128), hi, tot)
        after(3)
        digits("ty", 0, TY, V("ki", 0, TY), hi, tot)
        quant("TQ", 192 * slot, 192 * slot + TY, whole("ty", 0, TY))
        mm(BB, kq(K_4), ("TQ", 192 * slot + 40, 192 * slot + TY))
        mm(BA, kq(K_16), ("TQ", 192 * slot, 192 * slot + 128))
        after(0)
        o4 = V("off", o4c, o4c + 32)
        ts(o4, PS(BB, 96, 128), K(6), OP.add)
        copy(V("off", o0, o0 + 8), PS(BA, 0, 8))
        after(4)
        add("v", [V("dh", 0, 512), V("dv", 0, 512), o4], [V("ht", 0, 512)],
            lambda: g.vector.tensor_tensor(T.ht[:, 0:512], T.dh[:, 0:512].indirect(ap(o4)), T.dv[:, 0:512], OP.add))
        after(1)
        quant(*E, whole("ht", 0, 128))

    def after1(k):
        if k == 2:
            uquant(1)
            grab(V("prow", 0, 128), V("pall", 0, 256), V("off", O_V, O_V + 8))
            act(sub("ty", 2, 8, TW), IDN, FN.Copy, None, 16.0)
            kquant(K_4)
        if k == 3:
            kquant(K_SB)
            for b in range(2):
                ts(V(("ebq", "fl")[b], 0, 128), V("lrv", 0, 128), K(b), OP.is_equal)
                ts(V(("ea", "gm1")[b], 0, 128), V("prow", 0, 128), K(b), OP.is_equal)
        if k == 0:
            ts(C(14), C(13), K(0), OP.is_equal, BIG, OP.mult)
            for b in range(2):
                scan(V(("sc1", "sc2")[b], 0, 128), V(("ea", "gm1")[b], 0, 128), V(("ebq", "fl")[b], 0, 128), 0.0, OP.max, OP.max)
                act(V("junk", 0, 128), V(("ebq", "fl")[b], 0, 128), FN.Copy, None, None, C(8 + b))
        if k == 4:
            ts(V("tq", 0, 128), V("tp", 0, 128), C(14), OP.subtract)
            for b in range(2):
                count(("sc1", "sc2")[b], 128, 1.0, None, C(10 + b))
            for t, c in enumerate((-2.0 ** 30, 0.0, 2.0 ** 29, -2.0 ** 23)):
                act(sub("kt", t, 128 * K_C, 128 * K_C + 128), V("bm", 0, 128), FN.Copy, None, c)
        if k == 1:
            ts(sub("ct", 1, 128, 256), IDN, C(14), OP.mult, 1.0 / BIG, OP.mult)
            ts(C(15), C(13), K(0), OP.not_equal)
    F1 = ("W1", 128, 256)
    uquant(3)
    grab(V("r1", 64, 128), V("rr", 128, 256), V("ofr", 0, 4))
    pick(("W1", 192, 256), ("L0", 0, 128), 0, 4, "ofr")
    front(F1, 1, K_B, C(12), C(13), 3, O_P1, O_4, ("E1", 0, 128), after1)
    iota(V("par", 0, 256), [[1, 256]], 0, 0)
    dma("s", "dp1", [C(13)], [], lambda: T.pa[:, 256:384], lambda: T.col[:, 13:14])

    def gap1(k):
        if k == 0:
            row(3, BB)
            act(V("ebq", 0, 128), IDN, FN.Copy, None, C(15))
            pick(("PAR1", 0, 128), F1, O_P1, O_P1 + 8)
        if k == 3:
            ts(V("ea", 0, 128), PS(BB, 0, 128), K(0), OP.is_equal)
        if k == 1:
            scan(V("sc1", 0, 128), V("ea", 0, 128), V("ebq", 0, 128), 0.0, OP.max, OP.max)
            count("sc1", 128, 1.0, None, C(18))
            kquant(K_C)
        if k == 4:
            copy(V("k2", 0, 2), V("ki", 6, 8))
            copy(V("k2", 2, 4), V("ki", 0, 2))
        if k == 2:
            ts(sub("ts", 2, 0, 8), K8, C(15), OP.mult, 192.0, OP.mult)
            memset(sub("ct", 0, 64, 128, 0, 64), 1.0)
            memset(sub("ct", 0, 0, 64, 64, 128), 1.0)
            quant("WQ", 0, 256, whole("wt", 0, 256))
    choose(1, ("E1", 0, 128), K_SB, "tq", 2, 42, O_L1, gap1)
    pick(("SN1", 0, 64), ("E1", 0, 128), O_L1, O_L1 + 4)
    sent += send(1, ("SN1", 0, 64), ("W2", 160, 224), rank ^ PART[1])
    grab(V("lr1", 0, 64), NUM, V("off", O_L1, O_L1 + 4))
    settle(O_L1 + 4, 42)
    pick(("W2", 128, 160), ("E1", 0, 128), O_L1 + 2, O_L1 + 4)
    pick(("W2", 224, 256), ("E1", 0, 128), O_L1, O_L1 + 2)

    ts(V("eqi", 64, 128), V("lr1", 0, 64), C(18), OP.is_equal)
    pick(("PR1", 0, 128), ("PAR1", 0, 128), O_L1, O_L1 + 8)
    scan(V("sc", 0, 192), V("eqi", 64, 256), V("eqi", 64, 256), 0.0, OP.max, OP.max)
    count("sc", 192, 1.0, C(19), C(20))
    grab(V("lr0", 0, 128), NUM, V("off", O_L0, O_L0 + 8))
    add("v", [V("prow", 0, 128), V("off", O_V, O_V + 8)], [V("par", 0, 256)],
        lambda: g.vector.tensor_copy(T.par[:, 0:256].indirect(T.off[:, O_V:O_V + 8]), T.prow[:, 0:128]))
    dma("s", "dp0", [V("par", 0, 256)], [], lambda: T.pa[:, 0:256], lambda: T.par[0:1, 0:256])

    def after2(k):
        if k == 2:
            digits("ts", 0, 8, K8, C(19), C(20))
            later(0, 0)
        if k == 3:
            pend.append(carry("ts", 7, 128, 0, O_S1, 8))
            later(0, 1)
        if k == 0:
            row(5, BC)
            ts(C(23), C(22), K(0), OP.not_equal)
            later(0, 2)
            pend.pop()()
        if k == 4:
            ts(sub("ts", 2, 0, 4), V("k2", 0, 4), C(23), OP.mult, 128.0, OP.mult)
            ts(V("eqi", 0, 128), PS(BC, 0, 128), K(0), OP.is_equal)
        if k == 1:
            scan(V("sc", 0, 256), V("eqi", 0, 256), V("eqi", 0, 256), 0.0, OP.max, OP.max)
            pick(("PAR2", 0, 128), ("W2", 128, 256), O_P2, O_P2 + 8)
    F2, E2 = ("W2", 128, 256), ("W2", 256, 384)
    front(F2, 2, K_C, C(21), C(22), 5, O_P2, O_4 + 32, E2, after2)
    dma("s", "dp2", [C(22)], [], lambda: T.pa[:, 384:448], lambda: T.col[0:64, 22:23])

    count("sc", 256, 1.0, C(24), C(25))
    opend(("PAR2", 0, 128), K_E1, True)
    opend(E2, K_E1, False)
    digits("ts", 0, 4, V("k2", 0, 4), C(24), C(25))
    fin = carry("ts", 6, 128, BD, O_S2, 4)
    anew(("W2", 0, 128), True)
    fin()
    opend(("PR1", 0, 128), K_E1, True)
    pick(("W1", 256, 320), ("W2", 0, 384), O_S2, O_S2 + 4)
    opend(("W1", 192, 320), K_E1, False)
    anew(("W1", 0, 128), True)
    later(1, 0)
    pick(("SND", 0, 64), ("W1", 64, 320), O_S1 + 4, O_S1 + 8)
    sent += send(2, ("SND", 0, 64), ("W0", 384, 448), rank ^ PART[0])
    later(1, 1)
    pick(("W0", 448, 512), ("W1", 64, 320), O_S1, O_S1 + 4)

    later(1, 2)
    pick(("PR0", 0, 128), ("PAR0", 0, 128), O_L0, O_L0 + 8)
    opend(("PR0", 0, 128), K_E1, True)
    for b in range(2):
        ts(sub("ts", 2, 8 * b, 8 * b + 8), K8, C(8 + b), OP.mult, 384.0, OP.mult)
    digits("ts", 0, 8, K8, C(26), C(27))
    ts(C(30), C(29), 128.0, OP.is_ge, 128.0, OP.mult)
    digits("ts", 8, 16, K8, C(28), C(29))
    ts(sub("ts", 3, 8, 16), K8, C(30), OP.mult)
    carry("ts", 8, 128, BC, O_S0, 16)()
    opend(("W0", 384, 512), K_E1, False)
    anew(("W0", 0, 128), True)
    for h in range(2):
        pick(("FIN", 128 * h, 128 * h + 128), ("W0", 0, 512), O_S0 + 8 * h, O_S0 + 8 * h + 8)
        for o in range(2):
            mm(BA + 2 * h + o, ("WQ", 128 * o, 128 * o + 128), ("FIN", 128 * h, 128 * h + 128))
    dma("s", "doc", [V("qFIN", 0, 256)], [], lambda: T.oc[:, :], lambda: T.qFIN[:, 0:256].bitcast(dt.uint8))
    for k in range(4):
        dma("s", "ds%d" % k, [V("sFIN", 0, 256)], [],
            lambda k=k: T.osc[4 * k:4 * k + 4, :], lambda k=k: T.sFIN[32 * k:32 * k + 4, 0:256])
    for h in range(2):
        act(V("ysb", 128 * h, 128 * h + 128), PS(BA + 2 * h, 0, 128), FN.Copy)
        copy(V("ysb", 256 + 128 * h, 384 + 128 * h), PS(BB + 2 * h, 0, 128))
    dma("a", "dy0", [V("ysb", 0, 512)], [], lambda: T.y[:, :], lambda: T.ysb[:, :])

    assert sorted(ISSUE) == list(range(len(ops)))
    ops = [ops[n] for n in ISSUE]
    know = {q: {} for q in queue}
    for n, o in enumerate(ops):
        o["clock"] = o["q"] if o["kind"] == "c" else n
        o["waits"] = []
        if o["kind"] == "x":
            o["after"] = {n: n}
            continue
        need = {}
        for m in range(n):
            e = ops[m]
            if e["kind"] == "r" or (e["q"] == "p" and o["q"] == "p"):
                continue
            hit = any(clash(a, b) for a in o["r"] + o["w"] for b in e["w"]) or any(clash(a, b) for a in o["w"] for b in e["r"])
            if not hit and e["q"] != o["q"]:
                hit = any(a[0] == "ps" and clash(a, b) for a in o["r"] for b in e["r"])
            if hit:
                need[e["clock"]] = m
        k = know[o["q"]]
        for m in sorted(need.values(), reverse=True):
            e = ops[m]
            if k.get(e["clock"], -1) < m:
                o["waits"].append(m)
                e["inc"] = True
                for c, i in e["after"].items():
                    k[c] = max(k.get(c, -1), i)
        o["after"] = dict(k)
        o["after"][o["clock"]] = n
    cnt = {q: 0 for q in queue}
    for o in ops:
        if o["kind"] == "c" and o.get("inc"):
            cnt[o["q"]] += 1
            o["sem"] = ("c" + o["q"], cnt[o["q"]])
        if o["kind"] == "d":
            o["sem"] = (o["sem"], 16)
    for o in ops:
        if o["kind"] == "x":
            continue
        for m in o["waits"]:
            queue[o["q"]].wait_ge(T.sem[ops[m]["sem"][0]], ops[m]["sem"][1])
        ins = o["fn"]()
        if o["kind"] == "d":
            ins.then_inc(T.sem[o["sem"][0]], 16)
        elif o.get("inc"):
            ins.then_inc(T.sem[o["sem"][0]], 1)
    for o in ops:
        if o["kind"] == "d" and not o.get("inc"):
            queue[o["q"]].wait_ge(T.sem[o["sem"][0]], 16)
    g.wait_ge(T.sem.snt, sent)
